import numpy as np, ml_dtypes
CORES = [2,3,42,43,82,83,122,123]
N = 8
import mx_ref
BF = ml_dtypes.bfloat16
def cols(t, e):
    v = np.concatenate([t.reshape(128, -1, 4), np.zeros((128, 1, 4), BF)], axis=1)
    return np.ascontiguousarray(v[:, e]).reshape(128, -1)
def cut(t, i, w=512):
    return t[:, w * i:w * i + w]
def f(rng, *shape):
    return mx_ref.flush((rng.standard_normal(shape, dtype=np.float32) * np.exp2(rng.integers(-2, 3, shape[:-1] + (1,)))).astype(BF))
def wide(rng, *shape, cols=0):
    v = rng.standard_normal(shape, dtype=np.float32) * np.exp2(rng.integers(-12, 13, shape)).astype(np.float32)
    if cols: v *= np.repeat(np.exp2(rng.integers(-cols, cols + 1, shape[:-2] + (1, shape[-1] // 4))) * (rng.random(shape[:-2] + (1, shape[-1] // 4)) > 0.0625), 4, axis=-1).astype(np.float32)
    return mx_ref.flush(v.astype(BF))
P, K, R, O = 256, 96, 4, 3
PART = [1, 2, 4, 1]
def scores(c, qt):
    k = mx_ref.quantize(np.concatenate([qt[r][:, :4 * R] for r in range(N)], axis=1))
    s = [mx_ref.matmul(mx_ref.quantize(cut(c[q], i)), k) for q in range(N) for i in range(P // 128)]
    return np.concatenate(s).reshape(N * P, N, R)
def play(s):
    held, use, out = np.arange(N * P).reshape(N, P), np.zeros((N, P), np.float32), []
    for t in range(R):
        left = []
        for r in range(N):
            v = s[held[r], r, t]
            use[r] = use[r] + v * v
            left.append(np.argsort(use[r], kind="stable")[:K])
        new = held.copy()
        for r in range(N):
            p = r ^ PART[t]
            new[r, left[r]] = held[p, left[p]]
            use[r, left[r]] = 0
        held = new
        out.append(held)
    return np.stack(out)
def fit(s):
    a = np.abs(s)
    return bool(np.isfinite(a).all() and ((a == 0) | (a >= 2.0 ** -60) & (a <= 2.0 ** 60)).all())
def times(t, v):
    return mx_ref.flush((t.astype(np.float32) * np.asarray(v, np.float32)).astype(BF))
def plain(rng):
    q = np.array(f(rng, N, 128, 512))
    q[:, :, 4 * R:] = 0
    return {"c": f(rng, N, 128, 4 * P), "qt": q, "w": f(rng, N, 128, 512 * O)}
def first(make, good=None):
    for i in range(50):
        d = make()
        s = scores(d["c"], d["qt"])
        if fit(s) and (good is None or good(s)): return d
    raise RuntimeError("no draw of 50 is fit")
def athome(s):
    h, a = play(s), np.ones((N, R + 1, P), bool)
    for r in range(N):
        for t in range(R): a[r, t + 1] = np.isin(np.arange(P * r, P * r + P), h[t, r])
    return a
def setup_inputs(rng):
    return first(lambda: plain(rng))
def setup_inputs_sides(rng):
    top = np.arange(128) < 64
    def make():
        d = plain(rng)
        half = np.stack([rng.permutation(P) < P // 2 for r in range(N)])
        d["c"] = times(d["c"], np.repeat(half[:, None, :] == top[None, :, None], 4, axis=2))
        for t in range(R):
            g = np.where(top == (PART[t] == 1), 1.0, 2.0 ** -6) * 4.0 ** t
            d["qt"][:, :, 4 * t:4 * t + 4] = times(d["qt"][:, :, 4 * t:4 * t + 4], g[None, :, None])
        return d
    def good(s):
        a = athome(s)
        return bool((~a[:, :-1] & a[:, 1:]).any(axis=(1, 2)).all())
    return first(make, good)
def setup_inputs_ties(rng):
    def make():
        d = plain(rng)
        d["c"] = np.stack([times(cols(d["c"][r], rng.integers(0, 6, P)), np.repeat(1 - 2 * rng.integers(0, 2, P), 4)) for r in range(N)])
        return d
    def good(s):
        for r in range(N):
            v = s[P * r:P * r + P, r, 0]
            u = np.sort(v * v)
            if u[K - 1] != u[K]: return False
        return True
    return first(make, good)
def setup_inputs_shrink(rng):
    low = np.arange(N) >= N - N // 4
    def make():
        d = plain(rng)
        size = np.exp2(np.where(low, -30.0, 23.0)[:, None] + 2 * rng.random((N, P))) * (1 - 2 * rng.integers(0, 2, (N, P)))
        d["c"] = ((1 + rng.random((N, 128, 4 * P))) * np.repeat(size, 4, axis=1)[:, None, :]).astype(np.float32).astype(BF)
        on = ~low[:, None] | np.stack([rng.permutation(128) < 2 for r in range(N)])
        for t in range(R):
            g = np.exp2(np.where(low, 8.0 * (R - 1 - t) - 30.0, 21.0 - 8.0 * t))
            d["qt"][:, :, 4 * t:4 * t + 4] = ((1 + rng.random((N, 128, 4))) * (g[:, None] * on)[:, :, None]).astype(np.float32).astype(BF)
        return d
    def good(s):
        h, a, b = play(s), np.zeros(N, bool), np.zeros(N, bool)
        for r in range(N):
            at, use, since = np.arange(P * r, P * r + P), np.zeros(P, np.float32), np.zeros(P, int)
            if low[r] and np.abs(s[at, r, R - 1]).max() > 2.0 ** -50 or not low[r] and np.abs(s[at, r, 0]).min() < 2.0 ** 50: return False
            for t in range(R):
                v = s[at, r]
                use = use + v[:, t] * v[:, t]
                sums = np.concatenate([np.zeros((P, 1), np.float32), np.cumsum(v * v, axis=1)], axis=1)
                diff = sums[:, t + 1] - sums[np.arange(P), since]
                a[r] |= (np.argsort(use, kind="stable")[:K] != np.argsort(diff, kind="stable")[:K]).any()
                b[r] |= np.sort(use)[K - 1] > 1e30
                moved = h[t, r] != at
                at = h[t, r]
                use[moved] = 0
                since[moved] = t + 1
        return bool(2 * a.sum() > N and 2 * b.sum() > N)
    return first(make, good)
def setup_inputs_turn(rng):
    on = (np.arange(128) // (128 // N))[None, :] == np.arange(N)[:, None]
    def make():
        d = plain(rng)
        d["c"] = times(d["c"], np.where(on, 2.0 ** -8, 1.0)[:, :, None])
        d["qt"] = times(d["qt"], on[:, :, None])
        return d
    return first(make, lambda s: bool((~athome(s)).any(axis=1).all()))
def setup_inputs_spread(rng):
    return first(lambda: {**plain(rng), "c": wide(rng, N, 128, 4 * P, cols=6)})
def check_inputs(d):
    b = []
    for k in ("c", "qt", "w"):
        v = np.abs(d[k].astype(np.float32))
        if not (np.isfinite(v).all() and ((v == 0) | (v >= 2.0 ** -30) & (v <= 2.0 ** 30)).all()): b.append("a value of " + k)
    if (d["qt"][:, :, 4 * R:].astype(np.float32) != 0).any(): b.append("qt has numbers behind its first R columns")
    if not b and not fit(scores(d["c"], d["qt"])): b.append("a score")
    return b
def reference(c, qt, w):
    held = play(scores(c, qt))
    every = np.concatenate([c[q] for q in range(N)], axis=1)
    y = np.zeros((N, 128, R * O * P), np.float32)
    for r in range(N):
        u, at = np.unique(held[:, r].reshape(-1), return_inverse=True)
        at = at.reshape(R, P)
        q = mx_ref.quantize(cols(every, np.concatenate([u, np.full(-len(u) % 4, -1)])))
        for o in range(O):
            z = mx_ref.matmul(mx_ref.quantize(cut(w[r], o)), q)
            for t in range(R):
                i = (t * O + o) * P
                y[r, :, i:i + P] = z[:, at[t]]
    return {"y": y}

@@ -1,0 +1,380 @@
+from concourse.mybir import dt, AluOpType as A, AxisListType, ActivationFunctionType as AF
+
+P, K, R, O = 256, 96, 4, 3
+PART = [1, 2, 4, 1]
+NS = [P + K * t for t in range(R + 1)]
+
+SCRATCH = {
+    "cb": ("sbuf", [128, 4 * P], "bfloat16"),
+    "qb": ("sbuf", [128, 512], "bfloat16"),
+    "wb": ("sbuf", [128, 512 * O], "bfloat16"),
+    "qc": ("sbuf", [128, 128], "float8_e4m3fn_x4"),
+    "qs": ("sbuf", [128, 128], "uint8"),
+    "qrc": ("sbuf", [128, 128 * R], "float8_e4m3fn_x4"),
+    "qrs": ("sbuf", [128, 128 * R], "uint8"),
+    "wtc": ("sbuf", [128, 128 * O], "float8_e4m3fn_x4"),
+    "wts": ("sbuf", [128, 128 * O], "uint8"),
+    "w4c": ("sbuf", [128, 128], "float8_e4m3fn_x4"),
+    "w4s": ("sbuf", [128, 128], "uint8"),
+    "qoff": ("sbuf", [128, 8 * R], "uint16"),
+    "wr": ("sbuf", [128, NS[3]], "float32"),
+    "wc": ("sbuf", [128, NS[3]], "float32"),
+    "sq": ("sbuf", [128, 512], "float32"),
+    "u64": ("sbuf", [128, 64], "float32"),
+    "t4": ("sbuf", [128, 64], "float32"),
+    "rr": ("sbuf", [128, P], "float32"),
+    "mm": ("sbuf", [128, P], "float32"),
+    "pr": ("sbuf", [128, P], "float32"),
+    "p2": ("sbuf", [128, 8], "float32"),
+    "iot": ("sbuf", [128, NS[3]], "float32"),
+    "c0": ("sbuf", [128, 264], "float32"),
+    "c1": ("sbuf", [128, P], "float32"),
+    "dump": ("sbuf", [128, 264], "float32"),
+    "kk": ("sbuf", [128, 8], "float32"),
+    "qi": ("sbuf", [128, 8], "int32"),
+    "r8": ("sbuf", [128, 8], "float32"),
+    "off": ("sbuf", [128, 8], "uint16"),
+    "srow": ("sbuf", [128, 128], "bfloat16"),
+    "srowf": ("sbuf", [128, 128], "float32"),
+    "win": ("sbuf", [128, 512], "bfloat16"),
+    "winf": ("sbuf", [128, 512], "float32"),
+    "tt": ("sbuf", [128, 384], "bfloat16"),
+    "ttf": ("sbuf", [128, 384], "float32"),
+    "a12": ("sbuf", [128, 16], "float32"),
+    "a6": ("sbuf", [128, 8], "float32"),
+    "lst": ("sbuf", [128, 8], "uint16"),
+    "s8": ("sbuf", [128, 32], "float32"),
+    "qj": ("sbuf", [128, 8], "int32"),
+    "k8": ("sbuf", [128, 8], "float32"),
+    "n8": ("sbuf", [128, 8], "float32"),
+    "e8": ("sbuf", [128, 8], "float32"),
+    "hl": ("sbuf", [128, 8], "uint16"),
+    "xx": ("sbuf", [128, 32], "float32"),
+    "yy": ("sbuf", [128, 64], "float32"),
+    "zz": ("sbuf", [128, 64], "float32"),
+    "fl": ("sbuf", [128, 16], "uint16"),
+    "fy00": ("sbuf", [128, 8], "uint16"),
+    "fy10": ("sbuf", [128, 8], "uint16"),
+    "fy01": ("sbuf", [128, 8], "uint16"),
+    "fy11": ("sbuf", [128, 8], "uint16"),
+}
+for _t in range(R):
+    SCRATCH["w%dc" % _t] = ("sbuf", [128, NS[_t]], "float8_e4m3fn_x4")
+    SCRATCH["w%ds" % _t] = ("sbuf", [128, NS[_t]], "uint8")
+    SCRATCH["out%dc" % _t] = ("sbuf", [128, K], "float8_e4m3fn_x4")
+    SCRATCH["out%ds" % _t] = ("sbuf", [128, K], "uint8")
+    SCRATCH["yb%d" % _t] = ("sbuf", [128, O * P], "float32")
+for _o in range(O):
+    SCRATCH["yp%d" % _o] = ("sbuf", [128, NS[4]], "float32")
+for _b in range(8):
+    SCRATCH["ps%d" % _b] = ("psum", [128, 512], "float32")
+
+NDMA = 40
+SEMAPHORES = ["sg", "sv", "ss", "st"] + ["d%d" % i for i in range(NDMA)]
+for _t in range(R):
+    SEMAPHORES += ["ac%d" % _t, "as%d" % _t, "lc%d" % _t, "ls%d" % _t]
+
+
+def rank_program(g, core, T, topo):
+    rank = T.rank_of(core)
+    if rank is None:
+        return
+    Q = {"g": g, "v": g.vector, "s": g.scalar, "t": g.tensor, "y": g.sync}
+    own = {"g": "sg", "v": "sv", "s": "ss", "t": "st"}
+    PSB = ["ps%d" % i for i in range(8)]
+    count = {}
+    waited = {q: {} for q in Q}
+    recs = {}
+    ndma = [0]
+
+    def rg(b, c0, c1, p0=0, p1=128, lane=None):
+        return (b, c0, c1, p0, p1, lane)
+
+    def meets(a, b):
+        if a[0] in PSB:
+            return True
+        if a[5] is not None and b[5] is not None and a[5] != b[5]:
+            return False
+        return a[1] < b[2] and b[1] < a[2] and a[3] < b[4] and b[3] < a[4]
+
+    def covers(a, b):
+        return a[0] in PSB or (a[5] is None and a[1] <= b[1] and a[2] >= b[2] and a[3] <= b[3] and a[4] >= b[4])
+
+    def need(q, reads, writes):
+        w = {}
+        for regs, wr in ((reads, False), (writes, True)):
+            for r in regs:
+                for (x, xq, sem, n, xw) in recs.get(r[0], []):
+                    if not (wr or xw) or not meets(r, x):
+                        continue
+                    if wr and not xw and xq == q and q != "y":
+                        continue
+                    if r[0] in PSB and xq == q:
+                        continue
+                    w[sem] = max(w.get(sem, 0), n)
+        for sem in w:
+            if waited[q].get(sem, 0) < w[sem]:
+                Q[q].wait_ge(T.sem[sem], w[sem])
+                waited[q][sem] = w[sem]
+
+    def note(q, sem, n, reads, writes):
+        for r in writes:
+            recs[r[0]] = [e for e in recs.get(r[0], []) if not covers(r, e[0])]
+        for r in writes:
+            recs.setdefault(r[0], []).append((r, q, sem, n, True))
+        for r in reads:
+            recs.setdefault(r[0], []).append((r, q, sem, n, False))
+
+    def do(q, call, reads, writes):
+        need(q, reads, writes)
+        if q == "g" and count.get("sg", 0) > waited["g"].get("sg", 0):
+            g.wait_ge(T.sem.sg, count["sg"])
+            waited["g"]["sg"] = count["sg"]
+        ins = call()
+        sem = own[q]
+        count[sem] = count.get(sem, 0) + 1
+        ins.then_inc(T.sem[sem], 1)
+        note(q, sem, count[sem], reads, writes)
+
+    def dma(q, out, in_, reads, writes):
+        need(q, reads, writes)
+        sem = "d%d" % ndma[0]
+        ndma[0] += 1
+        Q[q].dma_start(out, in_).then_inc(T.sem[sem], 16)
+        count[sem] = 16
+        note("y" if q == "y" else q + "d", sem, 16, reads, writes)
+
+    def cp(q, ob, oc, ib, ic, p=(0, 128), ip=None):
+        ip = ip or p
+        o = T[ob][p[0]:p[1], slice(*oc)]
+        i = T[ib][ip[0]:ip[1], slice(*ic)]
+        rd = [rg(ib, ic[0], ic[1], ip[0], ip[1])]
+        wr = [rg(ob, oc[0], oc[1], p[0], p[1], (oc[0] % oc[2]) if len(oc) > 2 else None)]
+        if q == "v":
+            do("v", lambda: g.vector.tensor_copy(o, i), rd, wr)
+        else:
+            do("s", lambda: g.scalar.activation(o, i, AF.Copy), rd, wr)
+
+    def ts(out, in0, s1, s2, op0, op1, rd, wr):
+        if op1 is None:
+            do("v", lambda: g.vector.tensor_scalar(out, in0, s1, None, op0), rd, wr)
+        else:
+            do("v", lambda: g.vector.tensor_scalar(out, in0, s1, s2, op0, op1), rd, wr)
+
+    def tt(out, a, b, op, rd, wr):
+        do("v", lambda: g.vector.tensor_tensor(out, a, b, op), rd, wr)
+
+    def fill(b, c0, c1, v, p0=0, p1=128):
+        do("v", lambda: g.vector.memset(T[b][p0:p1, c0:c1], v), [], [rg(b, c0, c1, p0, p1)])
+
+    def tr(ob, o0, ib, i0, n):
+        do("v", lambda: g.vector.transpose(T[ob][:, o0:o0 + n], T[ib][:, i0:i0 + n]), [rg(ib, i0, i0 + n)], [rg(ob, o0, o0 + n)])
+
+    def mm(bank, lc, l0, rc, r0, n):
+        lh, ls, rh, rs = T[lc + "c"], T[lc + "s"], T[rc + "c"], T[rc + "s"]
+        do("t", lambda: g.tensor.matmul_mx(T[bank][:, 0:n], lh[:, l0:l0 + 128], ls[:, l0:l0 + 128], rh[:, r0:r0 + n], rs[:, r0:r0 + n], True, True),
+           [rg(lc + "c", l0, l0 + 128), rg(lc + "s", l0, l0 + 128), rg(rc + "c", r0, r0 + n), rg(rc + "s", r0, r0 + n)], [rg(bank, 0, 512)])
+
+    def square(ob, o0, bank, i0, n):
+        do("s", lambda: g.scalar.activation(T[ob][:, o0:o0 + n], T[bank][:, i0:i0 + n], AF.Square), [rg(bank, 0, 512)], [rg(ob, o0, o0 + n)])
+
+    def pick_query(t):
+        ol = T.qoff[:, 8 * t:8 * t + 8]
+        do("v", lambda: g.vector.tensor_copy(T.qrc[:, 128 * t:128 * t + 128].bitcast(dt.uint32), T.qc[:, 0:128].bitcast(dt.uint32).indirect(ol)),
+           [rg("qc", 0, 128), rg("qoff", 8 * t, 8 * t + 8)], [rg("qrc", 128 * t, 128 * t + 128)])
+        do("s", lambda: g.scalar.activation(T.qrs[:, 128 * t:128 * t + 128], T.qs[:, 0:128].indirect(ol), AF.Copy),
+           [rg("qs", 0, 128), rg("qoff", 8 * t, 8 * t + 8)], [rg("qrs", 128 * t, 128 * t + 128)])
+
+    def copy_slots(frm, to, c0, c1):
+        for k in ("c", "s"):
+            a, b = frm + k, to + k
+            i, o = T[a][:, c0:c1], T[b][:, c0:c1]
+            if k == "c":
+                i, o = i.bitcast(dt.uint8), o.bitcast(dt.uint8)
+            dma("y", o, i, [rg(a, c0, c1)], [rg(b, c0, c1)])
+
+    def lists(rel, ab, t):
+        tr("xx", 0, "s8", 0, 32)
+        for s in range(2):
+            for h in range(2):
+                cp("v", "yy", (32 * s + 16 * h, 32 * s + 16 * h + 16), "xx", (16 * s, 16 * s + 16))
+        tr("zz", 0, "yy", 0, 64)
+        for s in range(2):
+            if rel:
+                cp("v", "fl", (s, 16, 2), "zz", (32 * s, 32 * s + 8))
+        for s in range(2):
+            for h in range(2):
+                if ab:
+                    cp("v", "fy%d%d" % (h, t % 2), (s, 8, 2), "zz", (32 * s + 8 + h, 32 * s + 16, 2))
+
+    def slot_row(t):
+        b = "srowf" if t == 3 else "srow"
+        n = NS[t]
+        cp("v", "hl", (0, 8), "s8", (0, 8))
+        do("v", lambda: g.vector.tensor_copy(T[b][:, 0:128], T.iot[:, 0:n].indirect(T.hl[:, 0:8])), [rg("iot", 0, n), rg("hl", 0, 8)], [rg(b, 0, 128)])
+
+    dma("y", T.cb[:], T.c[:], [], [rg("cb", 0, 4 * P)])
+    dma("s", T.qb[:, 0:16], T.qt[:, 0:16], [], [rg("qb", 0, 16)])
+    dma("y", T.wb[:], T.w[:], [], [rg("wb", 0, 512 * O)])
+
+    def iota(b, c0, c1, pattern, base, cm, p0=0, p1=128):
+        do("g", lambda: g.iota(T[b][p0:p1, c0:c1], pattern, base, cm, allow_small_or_imprecise_dtypes=True), [], [rg(b, c0, c1, p0, p1)])
+
+    for a in range(4):
+        iota("s8", 0, 8, [[128 * (1 - 2 * (a // 2)), 2], [64 * (1 - 2 * (a % 2)), 2], [1, 2]], 64 * a, 2, 32 * a, 32 * a + 32)
+    iota("iot", 0, P, [[1, P]], -256, 0)
+    iota("p2", 0, 1, [[0, 1]], -256, 2)
+    iota("iot", P, NS[3], [[1, NS[3] - P]], 0, 0)
+
+    fill("qb", 16, 512, 0.0)
+    for t in range(R):
+        fill("qoff", 8 * t, 8 * t + 8, t)
+    do("v", lambda: g.vector.quantize_mx(T.qc[:, 0:128], T.qs[:, 0:128], T.qb[:, 0:512]), [rg("qb", 0, 512)], [rg("qc", 0, 128), rg("qs", 0, 128)])
+    pick_query(0)
+    fill("s8", 8, 32, 0.0)
+    lists(True, False, 0)
+    do("v", lambda: g.vector.quantize_mx(T.w0c[:, 0:P], T.w0s[:, 0:P], T.cb[:, 0:4 * P]), [rg("cb", 0, 4 * P)], [rg("w0c", 0, P), rg("w0s", 0, P)])
+    mm("ps0", "qr", 0, "w0", 0, P)
+    square("wr", 0, "ps0", 0, P)
+    do("v", lambda: g.vector.tensor_copy(T.pr[:, 0:P], T.iot[:, 0:P].indirect(T.fl[:, 0:16])), [rg("iot", 0, P), rg("fl", 0, 16)], [rg("pr", 0, P)])
+    ts(T.mm[:, 0:P], T.pr[:, 0:P], T.p2[:, 0:1], 1.0 - 2.0 ** -24, A.is_gt, A.max, [rg("pr", 0, P), rg("p2", 0, 1)], [rg("mm", 0, P)])
+    EPS = 2.0 ** -125
+    ts(T.wc[:, 0:P], T.wr[:, 0:P], EPS, None, A.max, None, [rg("wr", 0, P)], [rg("wc", 0, P)])
+    fill("c0", 256, 257, -1.0 / 16)
+    for t in range(1, R):
+        copy_slots("w0", "w%d" % t, 0, P)
+    copy_slots("w0", "w4", 0, 32)
+
+    def y_gather(q, t, o, h):
+        n = NS[t + 1]
+        b, s, f = "yb%d" % t, "yp%d" % o, "fy%d%d" % (h, t % 2)
+        out = T[b][:, P * o + h:P * o + P:2]
+        win = T[s][:, 0:n].indirect(T[f][:, 0:8])
+        rd, wr = [rg(s, 0, n), rg(f, 0, 8)], [rg(b, P * o, P * o + P, 0, 128, h)]
+        if q == "v":
+            do("v", lambda: g.vector.tensor_copy(out, win), rd, wr)
+        else:
+            do("s", lambda: g.scalar.activation(out, win, AF.Copy), rd, wr)
+
+    def y_store(t, o0, o1):
+        dma("y", T.y[:, P * (O * t + o0):P * (O * t + o1)], T["yb%d" % t][:, P * o0:P * o1], [rg("yb%d" % t, P * o0, P * o1)], [])
+
+    def new_products(t):
+        w = "w%d" % (t + 1)
+        r0 = NS[t] - 32 if t < 3 else 0
+        for o in range(O):
+            mm("ps%d" % (2 + o), "wt", 128 * o, w, r0, 128)
+
+    def new_copies(t, qs):
+        for o in range(O):
+            out, i = T["yp%d" % o][:, NS[t]:NS[t + 1]], T["ps%d" % (2 + o)][:, 32:128]
+            rd, wr = [rg("ps%d" % (2 + o), 0, 512)], [rg("yp%d" % o, NS[t], NS[t + 1])]
+            if qs[o] == "v":
+                do("v", lambda: g.vector.tensor_copy(out, i), rd, wr)
+            else:
+                do("s", lambda: g.scalar.activation(out, i, AF.Copy), rd, wr)
+
+    for t in range(R):
+        n = NS[t]
+        wn = "win" if t < 3 else "winf"
+        tb = "tt" if t < 3 else "ttf"
+        sr = "srow" if t < 3 else "srowf"
+        do("s", lambda: g.scalar.activation(T.u64[:, 0:64], T.wc[:, 0:n].indirect(T.fl[:, 0:4]), AF.Copy), [rg("wc", 0, n), rg("fl", 0, 16)], [rg("u64", 0, 64)])
+        tt(T.rr[:, 0:P], T.wc[:, 0:n].indirect(T.fl[:, 0:16]), T.mm[:, 0:P], A.mult, [rg("wc", 0, n), rg("fl", 0, 16), rg("mm", 0, P)], [rg("rr", 0, P)])
+        tr("t4", 0, "u64", 0, 64)
+        ts(T.c0[:, 0:P], T.rr[:, 0:P], T.t4[:, 0:1], 1.0 / 16, A.is_lt, A.mult, [rg("rr", 0, P), rg("t4", 0, 1)], [rg("c0", 0, P)])
+        do("s", lambda: g.scalar.activation(T.dump[:, 0:257], T.c0[:, 0:257], AF.Copy, accum_out=T.kk[:, 0:1]), [rg("c0", 0, 257)], [rg("dump", 0, 257), rg("kk", 0, 1)])
+        ts(T.c1[:, 0:P], T.rr[:, 0:P], T.t4[:, 32:33], 1.0 / 16, A.is_lt, A.mult, [rg("rr", 0, P), rg("t4", 32, 33)], [rg("c1", 0, P)])
+        do("v", lambda: g.vector.tensor_reduce(T.kk[:, 1:2], T.c1[:, 0:P], AxisListType.X, A.add), [rg("c1", 0, P)], [rg("kk", 1, 2)])
+        ts(T.qi[:, 0:2], T.kk[:, 0:2], -15.0 / 32, None, A.add, None, [rg("kk", 0, 2)], [rg("qi", 0, 2)])
+        tt(T.r8[:, 0:2], T.kk[:, 0:2], T.qi[:, 0:2], A.add, [rg("kk", 0, 2), rg("qi", 0, 2)], [rg("r8", 0, 2)])
+        cp("v", "r8", (2, 4), "r8", (0, 2), (64, 96), (96, 128))
+        cp("s", "r8", (2, 4), "r8", (0, 2), (0, 32), (32, 64))
+        cp("v", "r8", (2, 4), "r8", (0, 2), (96, 128), (64, 96))
+        cp("s", "r8", (2, 4), "r8", (0, 2), (32, 64), (0, 32))
+        cp("v", "r8", (4, 8), "r8", (0, 4), (0, 64), (64, 128))
+        cp("s", "r8", (4, 8), "r8", (0, 4), (64, 128), (0, 64))
+        if t == 0:
+            slot_row(0)
+            fill("win", 0, 208, 0.0)
+        ts(T.off[:, 0:8], T.r8[:, 0:8], 16.0, 16.0, A.mult, A.add, [rg("r8", 0, 8)], [rg("off", 0, 8)])
+        do("v", lambda: g.vector.tensor_copy(T[wn][:, 0:512].indirect(T.off[:, 0:8]), T[sr][:, 0:128]), [rg(sr, 0, 128), rg("off", 0, 8)], [rg(wn, 0, 512)])
+        tr(tb, 0, wn, 16, 192)
+        tr(tb, 192, wn, 0, 192)
+        tt(T.a12[:, 0:12], T[tb][:, 0:384:32], T[tb][:, 16:384:32], A.add, [rg(tb, 0, 384)], [rg("a12", 0, 12)])
+        tt(T.a6[:, 0:6], T.a12[:, 0:6], T.a12[:, 6:12], A.add, [rg("a12", 0, 12)], [rg("a6", 0, 6)])
+        ts(T.lst[:, 0:6], T.a6[:, 0:6], 256.0, None, A.add, None, [rg("a6", 0, 6)], [rg("lst", 0, 6)])
+        wc_, ws_, oc_, os_ = "w%dc" % t, "w%ds" % t, "out%dc" % t, "out%ds" % t
+        do("v", lambda: g.vector.tensor_copy(T[oc_][:, 0:K].bitcast(dt.uint32), T[wc_][:, 0:n].bitcast(dt.uint32).indirect(T.lst[:, 0:6])),
+           [rg(wc_, 0, n), rg("lst", 0, 6)], [rg(oc_, 0, K)])
+        do("s", lambda: g.scalar.activation(T[os_][:, 0:K], T[ws_][:, 0:n].indirect(T.lst[:, 0:6]), AF.Copy),
+           [rg(ws_, 0, n), rg("lst", 0, 6)], [rg(os_, 0, K)])
+        dst = T.cores[rank ^ PART[t]]
+        rid, pid, _ = topo.addr(dst)
+        nx = "w%d" % (t + 1)
+        l0 = n if t < 3 else 32
+        for k, b in (("c", oc_), ("s", os_)):
+            i, o = T[b][:, 0:K], T[nx + k][:, l0:l0 + K]
+            if k == "c":
+                i, o = i.bitcast(dt.uint8), o.bitcast(dt.uint8)
+            need("g", [rg(b, 0, K)], [])
+            g.remote_dma(o, i, T.sem["a%s%d" % (k, t)], T.sem["l%s%d" % (k, t)], pid, rid, topo.mask(core, dst))
+            came = len(topo.engines(dst, core))
+            count["l%s%d" % (k, t)] = len(topo.engines(core, dst))
+            count["a%s%d" % (k, t)] = came
+            note("r", "a%s%d" % (k, t), came, [], [rg(nx + k, l0, l0 + K)])
+
+        if t == 0:
+            pick_query(1)
+        if t < 3:
+            mm("ps0", "qr", 128 * (t + 1), "w%d" % t, 0, n)
+            square("sq", 0, "ps0", 0, n)
+        ts(T.qj[:, 0:8], T.r8[:, 0:8], 0.5, -0.25, A.mult, A.add, [rg("r8", 0, 8)], [rg("qj", 0, 8)])
+        ts(T.e8[:, 0:8], T.r8[:, 0:8], 11.5, None, A.is_lt, None, [rg("r8", 0, 8)], [rg("e8", 0, 8)])
+        tt(T.k8[:, 0:8], T.r8[:, 0:8], T.qj[:, 0:8], A.subtract, [rg("r8", 0, 8), rg("qj", 0, 8)], [rg("k8", 0, 8)])
+        ts(T.n8[:, 0:8], T.k8[:, 0:8], 16.0, float(n), A.mult, A.add, [rg("k8", 0, 8)], [rg("n8", 0, 8)])
+        tt(T.n8[:, 0:8], T.n8[:, 0:8], T.s8[:, 0:8], A.subtract, [rg("n8", 0, 8), rg("s8", 0, 8)], [rg("n8", 0, 8)])
+        tt(T.n8[:, 0:8], T.n8[:, 0:8], T.e8[:, 0:8], A.mult, [rg("n8", 0, 8), rg("e8", 0, 8)], [rg("n8", 0, 8)])
+        tt(T.s8[:, 0:8], T.s8[:, 0:8], T.n8[:, 0:8], A.add, [rg("s8", 0, 8), rg("n8", 0, 8)], [rg("s8", 0, 8)])
+        for a in range(4):
+            run = (8, 2, 4, 2)[a]
+            for c in range(0, 8, run):
+                o = 8 + (c ^ (2 * a))
+                cp("s", "s8", (o, o + run), "s8", (c, c + run), (32 * a, 32 * a + 32))
+        if t < 3:
+            slot_row(t + 1)
+            tt(T.wr[:, 0:n], T.wr[:, 0:n], T.sq[:, 0:n], A.add, [rg("wr", 0, n), rg("sq", 0, n)], [rg("wr", 0, n)])
+            ts(T.wc[:, 0:n], T.wr[:, 0:n], EPS, None, A.max, None, [rg("wr", 0, n)], [rg("wc", 0, n)])
+            fill("winf" if t == 2 else "win", 0, 208, 0.0)
+        lists(t < 3, True, t)
+        if t > 0:
+            new_copies(t - 1, "sss")
+            for o in range(O):
+                for h in range(2):
+                    y_gather("v" if o == 0 else "s", t - 1, o, h)
+            y_store(t - 1, 0, O)
+        if t == 0:
+            for o in range(O):
+                do("v", lambda: g.vector.quantize_mx(T.wtc[:, 128 * o:128 * o + 128], T.wts[:, 128 * o:128 * o + 128], T.wb[:, 512 * o:512 * o + 512]),
+                   [rg("wb", 512 * o, 512 * o + 512)], [rg("wtc", 128 * o, 128 * o + 128), rg("wts", 128 * o, 128 * o + 128)])
+                mm("ps%d" % (5 + o), "wt", 128 * o, "w0", 0, P)
+                out, i = T["yp%d" % o][:, 0:P], T["ps%d" % (5 + o)][:, 0:P]
+                do("s", lambda: g.scalar.activation(out, i, AF.Copy), [rg("ps%d" % (5 + o), 0, 512)], [rg("yp%d" % o, 0, P)])
+            pick_query(2)
+            pick_query(3)
+        if t < 3:
+            mm("ps1", "qr", 128 * (t + 1), nx, n - 32, 128)
+            square("wr", n, "ps1", 32, K)
+            ts(T.wc[:, n:n + K], T.wr[:, n:n + K], EPS, None, A.max, None, [rg("wr", n, n + K)], [rg("wc", n, n + K)])
+            for u in range(t + 2, R):
+                copy_slots(nx, "w%d" % u, n, n + K)
+        new_products(t)
+    new_copies(3, "svs")
+    for o in range(O):
+        y_gather("v", 3, o, 0)
+        y_gather("s", 3, o, 1)
+        y_store(3, o, o + 1)
+
+    for sem in count:
+        if waited["g"].get(sem, 0) < count[sem]:
+            g.wait_ge(T.sem[sem], count[sem])

@@ -3,76 +3,35 @@ from concourse.mybir import dt, AluOpType as A, AxisListType, ActivationFunction
 P, K, R, O = 256, 96, 4, 3
 PART = [1, 2, 4, 1]
 NS = [P + K * t for t in range(R + 1)]
+EPS = 2.0 ** -125
 
-SCRATCH = {
-    "cb": ("sbuf", [128, 4 * P], "bfloat16"),
-    "qb": ("sbuf", [128, 512], "bfloat16"),
-    "wb": ("sbuf", [128, 512 * O], "bfloat16"),
-    "qc": ("sbuf", [128, 128], "float8_e4m3fn_x4"),
-    "qs": ("sbuf", [128, 128], "uint8"),
-    "qrc": ("sbuf", [128, 128 * R], "float8_e4m3fn_x4"),
-    "qrs": ("sbuf", [128, 128 * R], "uint8"),
-    "wtc": ("sbuf", [128, 128 * O], "float8_e4m3fn_x4"),
-    "wts": ("sbuf", [128, 128 * O], "uint8"),
-    "w4c": ("sbuf", [128, 128], "float8_e4m3fn_x4"),
-    "w4s": ("sbuf", [128, 128], "uint8"),
-    "qoff": ("sbuf", [128, 8 * R], "uint16"),
-    "wr": ("sbuf", [128, NS[3]], "float32"),
-    "wc": ("sbuf", [128, NS[3]], "float32"),
-    "sq": ("sbuf", [128, 512], "float32"),
-    "u64": ("sbuf", [128, 64], "float32"),
-    "t4": ("sbuf", [128, 64], "float32"),
-    "rr": ("sbuf", [128, P], "float32"),
-    "mm": ("sbuf", [128, P], "float32"),
-    "pr": ("sbuf", [128, P], "float32"),
-    "p2": ("sbuf", [128, 8], "float32"),
-    "iot": ("sbuf", [128, NS[3]], "float32"),
-    "c0": ("sbuf", [128, 264], "float32"),
-    "c1": ("sbuf", [128, P], "float32"),
-    "dump": ("sbuf", [128, 264], "float32"),
-    "kk": ("sbuf", [128, 8], "float32"),
-    "qi": ("sbuf", [128, 8], "int32"),
-    "r8": ("sbuf", [128, 8], "float32"),
-    "off": ("sbuf", [128, 8], "uint16"),
-    "srow": ("sbuf", [128, 128], "bfloat16"),
-    "srowf": ("sbuf", [128, 128], "float32"),
-    "win": ("sbuf", [128, 512], "bfloat16"),
-    "winf": ("sbuf", [128, 512], "float32"),
-    "tt": ("sbuf", [128, 384], "bfloat16"),
-    "ttf": ("sbuf", [128, 384], "float32"),
-    "a12": ("sbuf", [128, 16], "float32"),
-    "a6": ("sbuf", [128, 8], "float32"),
-    "lst": ("sbuf", [128, 8], "uint16"),
-    "s8": ("sbuf", [128, 32], "float32"),
-    "qj": ("sbuf", [128, 8], "int32"),
-    "k8": ("sbuf", [128, 8], "float32"),
-    "n8": ("sbuf", [128, 8], "float32"),
-    "e8": ("sbuf", [128, 8], "float32"),
-    "hl": ("sbuf", [128, 8], "uint16"),
-    "xx": ("sbuf", [128, 32], "float32"),
-    "yy": ("sbuf", [128, 64], "float32"),
-    "zz": ("sbuf", [128, 64], "float32"),
-    "fl": ("sbuf", [128, 16], "uint16"),
-    "fy00": ("sbuf", [128, 8], "uint16"),
-    "fy10": ("sbuf", [128, 8], "uint16"),
-    "fy01": ("sbuf", [128, 8], "uint16"),
-    "fy11": ("sbuf", [128, 8], "uint16"),
-}
+SCRATCH = {"cb": ("sbuf", [128, 4 * P], "bfloat16"), "qb": ("sbuf", [128, 512], "bfloat16"), "wb": ("sbuf", [128, 512 * O], "bfloat16")}
+SEMAPHORES = ["sg", "sv", "ss", "st"] + ["d%d" % i for i in range(48)]
+for _b, _n in (("q", 128), ("qr", 128 * R), ("wt", 128 * O), ("w4", 128)):
+    SCRATCH[_b + "c"] = ("sbuf", [128, _n], "float8_e4m3fn_x4")
+    SCRATCH[_b + "s"] = ("sbuf", [128, _n], "uint8")
 for _t in range(R):
-    SCRATCH["w%dc" % _t] = ("sbuf", [128, NS[_t]], "float8_e4m3fn_x4")
-    SCRATCH["w%ds" % _t] = ("sbuf", [128, NS[_t]], "uint8")
-    SCRATCH["out%dc" % _t] = ("sbuf", [128, K], "float8_e4m3fn_x4")
-    SCRATCH["out%ds" % _t] = ("sbuf", [128, K], "uint8")
+    for _b, _n in (("w%d" % _t, NS[_t]), ("out%d" % _t, K)):
+        SCRATCH[_b + "c"] = ("sbuf", [128, _n], "float8_e4m3fn_x4")
+        SCRATCH[_b + "s"] = ("sbuf", [128, _n], "uint8")
     SCRATCH["yb%d" % _t] = ("sbuf", [128, O * P], "float32")
+    SCRATCH["cw%d" % _t] = ("sbuf", [128, 512], "float32")
+    SCRATCH["fy%d" % _t] = ("sbuf", [128, 16], "uint16")
+    SCRATCH["srow%d" % _t] = ("sbuf", [128, 128], "bfloat16" if _t < 3 else "float32")
+    SEMAPHORES += ["ac%d" % _t, "as%d" % _t, "lc%d" % _t, "ls%d" % _t]
 for _o in range(O):
     SCRATCH["yp%d" % _o] = ("sbuf", [128, NS[4]], "float32")
 for _b in range(8):
     SCRATCH["ps%d" % _b] = ("psum", [128, 512], "float32")
-
-NDMA = 40
-SEMAPHORES = ["sg", "sv", "ss", "st"] + ["d%d" % i for i in range(NDMA)]
-for _t in range(R):
-    SEMAPHORES += ["ac%d" % _t, "as%d" % _t, "lc%d" % _t, "ls%d" % _t]
+for _b, _n in (("wr", NS[3]), ("wc", NS[3]), ("sq", 512), ("u64", 64), ("t4", 64), ("rr", P), ("mm", P), ("pr", P), ("p2", 8), ("iot", P),
+               ("c0", 264), ("c1", P), ("dump", 264), ("kk", 8), ("r8", 8), ("winf", 512), ("ttf", 384), ("a12", 16), ("a6", 8), ("s8", 8),
+               ("dd0", P), ("dd1", P), ("dt0", P), ("fyf", 16)):
+    SCRATCH[_b] = ("sbuf", [128, _n], "float32")
+for _b, _n in (("win", 512), ("ttb", 384)):
+    SCRATCH[_b] = ("sbuf", [128, _n], "bfloat16")
+for _b, _n in (("qoff", 8 * R), ("off", 8), ("hl", 8), ("offd", 16), ("lst", 8), ("fl", 16)):
+    SCRATCH[_b] = ("sbuf", [128, _n], "uint16")
+SCRATCH["qi"] = ("sbuf", [128, 8], "int32")
 
 
 def rank_program(g, core, T, topo):
@@ -81,7 +40,6 @@ def rank_program(g, core, T, topo):
         return
     Q = {"g": g, "v": g.vector, "s": g.scalar, "t": g.tensor, "y": g.sync}
     own = {"g": "sg", "v": "sv", "s": "ss", "t": "st"}
-    PSB = ["ps%d" % i for i in range(8)]
     count = {}
     waited = {q: {} for q in Q}
     recs = {}
@@ -91,14 +49,14 @@ def rank_program(g, core, T, topo):
         return (b, c0, c1, p0, p1, lane)
 
     def meets(a, b):
-        if a[0] in PSB:
+        if a[0][:2] == "ps":
             return True
         if a[5] is not None and b[5] is not None and a[5] != b[5]:
             return False
         return a[1] < b[2] and b[1] < a[2] and a[3] < b[4] and b[3] < a[4]
 
     def covers(a, b):
-        return a[0] in PSB or (a[5] is None and a[1] <= b[1] and a[2] >= b[2] and a[3] <= b[3] and a[4] >= b[4])
+        return a[0][:2] == "ps" or (a[5] is None and a[1] <= b[1] and a[2] >= b[2] and a[3] <= b[3] and a[4] >= b[4])
 
     def need(q, reads, writes):
         w = {}
@@ -109,7 +67,7 @@ def rank_program(g, core, T, topo):
                         continue
                     if wr and not xw and xq == q and q != "y":
                         continue
-                    if r[0] in PSB and xq == q:
+                    if r[0][:2] == "ps" and xq == q:
                         continue
                     w[sem] = max(w.get(sem, 0), n)
         for sem in w:
@@ -164,26 +122,34 @@ def rank_program(g, core, T, topo):
     def tt(out, a, b, op, rd, wr):
         do("v", lambda: g.vector.tensor_tensor(out, a, b, op), rd, wr)
 
-    def fill(b, c0, c1, v, p0=0, p1=128):
-        do("v", lambda: g.vector.memset(T[b][p0:p1, c0:c1], v), [], [rg(b, c0, c1, p0, p1)])
+    def fill(b, c0, c1, v):
+        do("v", lambda: g.vector.memset(T[b][:, c0:c1], v), [], [rg(b, c0, c1)])
 
     def tr(ob, o0, ib, i0, n):
         do("v", lambda: g.vector.transpose(T[ob][:, o0:o0 + n], T[ib][:, i0:i0 + n]), [rg(ib, i0, i0 + n)], [rg(ob, o0, o0 + n)])
+
+    def pick(ob, o0, ib, n, lb, l0, k):
+        ol = T[lb][:, l0:l0 + k // 16]
+        c, s, oc, os_ = ib + "c", ib + "s", ob + "c", ob + "s"
+        lr = rg(lb, l0, l0 + k // 16)
+        do("v", lambda: g.vector.tensor_copy(T[oc][:, o0:o0 + k].bitcast(dt.uint32), T[c][:, 0:n].bitcast(dt.uint32).indirect(ol)), [rg(c, 0, n), lr], [rg(oc, o0, o0 + k)])
+        do("s", lambda: g.scalar.activation(T[os_][:, o0:o0 + k], T[s][:, 0:n].indirect(ol), AF.Copy), [rg(s, 0, n), lr], [rg(os_, o0, o0 + k)])
 
     def mm(bank, lc, l0, rc, r0, n):
         lh, ls, rh, rs = T[lc + "c"], T[lc + "s"], T[rc + "c"], T[rc + "s"]
         do("t", lambda: g.tensor.matmul_mx(T[bank][:, 0:n], lh[:, l0:l0 + 128], ls[:, l0:l0 + 128], rh[:, r0:r0 + n], rs[:, r0:r0 + n], True, True),
            [rg(lc + "c", l0, l0 + 128), rg(lc + "s", l0, l0 + 128), rg(rc + "c", r0, r0 + n), rg(rc + "s", r0, r0 + n)], [rg(bank, 0, 512)])
 
+    def quantize(ob, o0, n, ib):
+        c, s = T[ob + "c"], T[ob + "s"]
+        do("v", lambda: g.vector.quantize_mx(c[:, o0:o0 + n], s[:, o0:o0 + n], T[ib][:, 4 * o0:4 * (o0 + n)]),
+           [rg(ib, 4 * o0, 4 * (o0 + n))], [rg(ob + "c", o0, o0 + n), rg(ob + "s", o0, o0 + n)])
+
     def square(ob, o0, bank, i0, n):
         do("s", lambda: g.scalar.activation(T[ob][:, o0:o0 + n], T[bank][:, i0:i0 + n], AF.Square), [rg(bank, 0, 512)], [rg(ob, o0, o0 + n)])
 
-    def pick_query(t):
-        ol = T.qoff[:, 8 * t:8 * t + 8]
-        do("v", lambda: g.vector.tensor_copy(T.qrc[:, 128 * t:128 * t + 128].bitcast(dt.uint32), T.qc[:, 0:128].bitcast(dt.uint32).indirect(ol)),
-           [rg("qc", 0, 128), rg("qoff", 8 * t, 8 * t + 8)], [rg("qrc", 128 * t, 128 * t + 128)])
-        do("s", lambda: g.scalar.activation(T.qrs[:, 128 * t:128 * t + 128], T.qs[:, 0:128].indirect(ol), AF.Copy),
-           [rg("qs", 0, 128), rg("qoff", 8 * t, 8 * t + 8)], [rg("qrs", 128 * t, 128 * t + 128)])
+    def lift(c0, c1):
+        ts(T.wc[:, c0:c1], T.wr[:, c0:c1], EPS, None, A.max, None, [rg("wr", c0, c1)], [rg("wc", c0, c1)])
 
     def copy_slots(frm, to, c0, c1):
         for k in ("c", "s"):
@@ -193,64 +159,57 @@ def rank_program(g, core, T, topo):
                 i, o = i.bitcast(dt.uint8), o.bitcast(dt.uint8)
             dma("y", o, i, [rg(a, c0, c1)], [rg(b, c0, c1)])
 
-    def lists(rel, ab, t):
-        tr("xx", 0, "s8", 0, 32)
-        for s in range(2):
-            for h in range(2):
-                cp("v", "yy", (32 * s + 16 * h, 32 * s + 16 * h + 16), "xx", (16 * s, 16 * s + 16))
-        tr("zz", 0, "yy", 0, 64)
-        for s in range(2):
-            if rel:
-                cp("v", "fl", (s, 16, 2), "zz", (32 * s, 32 * s + 8))
-        for s in range(2):
-            for h in range(2):
-                if ab:
-                    cp("v", "fy%d%d" % (h, t % 2), (s, 8, 2), "zz", (32 * s + 8 + h, 32 * s + 16, 2))
+    def own_list(d):
+        tr("dt0", 0, d, 0, P)
+        ts(T.fl[:, 0:16], T.dt0[:, 0:P:16], 256.0, None, A.add, None, [rg("dt0", 0, P)], [rg("fl", 0, 16)])
 
-    def slot_row(t):
-        b = "srowf" if t == 3 else "srow"
-        n = NS[t]
-        cp("v", "hl", (0, 8), "s8", (0, 8))
-        do("v", lambda: g.vector.tensor_copy(T[b][:, 0:128], T.iot[:, 0:n].indirect(T.hl[:, 0:8])), [rg("iot", 0, n), rg("hl", 0, 8)], [rg(b, 0, 128)])
-
-    dma("y", T.cb[:], T.c[:], [], [rg("cb", 0, 4 * P)])
-    dma("s", T.qb[:, 0:16], T.qt[:, 0:16], [], [rg("qb", 0, 16)])
-    dma("y", T.wb[:], T.w[:], [], [rg("wb", 0, 512 * O)])
+    def by_list(out, ob, n, win, lb, k):
+        do("v", lambda: g.vector.tensor_copy(out, T[win][:, 0:P].indirect(T[lb][:, 0:k])), [rg(win, 0, P), rg(lb, 0, k)], [rg(ob, 0, n)])
 
     def iota(b, c0, c1, pattern, base, cm, p0=0, p1=128):
         do("g", lambda: g.iota(T[b][p0:p1, c0:c1], pattern, base, cm, allow_small_or_imprecise_dtypes=True), [], [rg(b, c0, c1, p0, p1)])
 
+    dma("y", T.cb[:], T.c[:], [], [rg("cb", 0, 4 * P)])
+    dma("s", T.qb[:, 0:16], T.qt[:, 0:16], [], [rg("qb", 0, 16)])
+    dma("y", T.wb[:], T.w[:], [rg("cb", 0, 4 * P)], [rg("wb", 0, 512 * O)])
     for a in range(4):
         iota("s8", 0, 8, [[128 * (1 - 2 * (a // 2)), 2], [64 * (1 - 2 * (a % 2)), 2], [1, 2]], 64 * a, 2, 32 * a, 32 * a + 32)
     iota("iot", 0, P, [[1, P]], -256, 0)
     iota("p2", 0, 1, [[0, 1]], -256, 2)
-    iota("iot", P, NS[3], [[1, NS[3] - P]], 0, 0)
+    for t in range(R):
+        iota("cw%d" % t, 16, 208, [[16, 6], [0, 2], [1, 16]], NS[t] - 256, 0)
+        iota("cw%d" % t, 208, 512, [[0, 304]], -1000, 0)
+        iota("cw%d" % t, 0, 16, [[0, 16]], -1000, 0)
 
     fill("qb", 16, 512, 0.0)
     for t in range(R):
         fill("qoff", 8 * t, 8 * t + 8, t)
-    do("v", lambda: g.vector.quantize_mx(T.qc[:, 0:128], T.qs[:, 0:128], T.qb[:, 0:512]), [rg("qb", 0, 512)], [rg("qc", 0, 128), rg("qs", 0, 128)])
-    pick_query(0)
-    fill("s8", 8, 32, 0.0)
-    lists(True, False, 0)
-    do("v", lambda: g.vector.quantize_mx(T.w0c[:, 0:P], T.w0s[:, 0:P], T.cb[:, 0:4 * P]), [rg("cb", 0, 4 * P)], [rg("w0c", 0, P), rg("w0s", 0, P)])
+    fill("c0", 256, 257, -1.0 / 16)
+    fill("win", 0, 208, 0.0)
+    cp("v", "offd", (0, 16, 2), "s8", (0, 8))
+    cp("v", "offd", (1, 16, 2), "s8", (0, 8))
+    cp("v", "hl", (0, 8), "s8", (0, 8))
+    by_list(T.dd0[:, 0:P], "dd0", P, "iot", "offd", 16)
+    own_list("dd0")
+    quantize("q", 0, 128, "qb")
+    pick("qr", 0, "q", 128, "qoff", 0, 128)
+    by_list(T.srow0[:, 0:128], "srow0", 128, "iot", "hl", 8)
+    quantize("w0", 0, P, "cb")
     mm("ps0", "qr", 0, "w0", 0, P)
     square("wr", 0, "ps0", 0, P)
-    do("v", lambda: g.vector.tensor_copy(T.pr[:, 0:P], T.iot[:, 0:P].indirect(T.fl[:, 0:16])), [rg("iot", 0, P), rg("fl", 0, 16)], [rg("pr", 0, P)])
+    by_list(T.pr[:, 0:P], "pr", P, "iot", "fl", 16)
     ts(T.mm[:, 0:P], T.pr[:, 0:P], T.p2[:, 0:1], 1.0 - 2.0 ** -24, A.is_gt, A.max, [rg("pr", 0, P), rg("p2", 0, 1)], [rg("mm", 0, P)])
-    EPS = 2.0 ** -125
-    ts(T.wc[:, 0:P], T.wr[:, 0:P], EPS, None, A.max, None, [rg("wr", 0, P)], [rg("wc", 0, P)])
-    fill("c0", 256, 257, -1.0 / 16)
+    lift(0, P)
     for t in range(1, R):
         copy_slots("w0", "w%d" % t, 0, P)
     copy_slots("w0", "w4", 0, 32)
 
     def y_gather(q, t, o, h):
         n = NS[t + 1]
-        b, s, f = "yb%d" % t, "yp%d" % o, "fy%d%d" % (h, t % 2)
+        b, s, f = "yb%d" % t, "yp%d" % o, "fy%d" % t
         out = T[b][:, P * o + h:P * o + P:2]
-        win = T[s][:, 0:n].indirect(T[f][:, 0:8])
-        rd, wr = [rg(s, 0, n), rg(f, 0, 8)], [rg(b, P * o, P * o + P, 0, 128, h)]
+        win = T[s][:, 0:n].indirect(T[f][:, 8 * h:8 * h + 8])
+        rd, wr = [rg(s, 0, n), rg(f, 8 * h, 8 * h + 8)], [rg(b, P * o, P * o + P, 0, 128, h)]
         if q == "v":
             do("v", lambda: g.vector.tensor_copy(out, win), rd, wr)
         else:
@@ -260,25 +219,17 @@ def rank_program(g, core, T, topo):
         dma("y", T.y[:, P * (O * t + o0):P * (O * t + o1)], T["yb%d" % t][:, P * o0:P * o1], [rg("yb%d" % t, P * o0, P * o1)], [])
 
     def new_products(t):
-        w = "w%d" % (t + 1)
-        r0 = NS[t] - 32 if t < 3 else 0
         for o in range(O):
-            mm("ps%d" % (2 + o), "wt", 128 * o, w, r0, 128)
+            mm("ps%d" % (2 + o), "wt", 128 * o, "w%d" % (t + 1), NS[t] - 32 if t < 3 else 0, 128)
 
     def new_copies(t, qs):
         for o in range(O):
-            out, i = T["yp%d" % o][:, NS[t]:NS[t + 1]], T["ps%d" % (2 + o)][:, 32:128]
-            rd, wr = [rg("ps%d" % (2 + o), 0, 512)], [rg("yp%d" % o, NS[t], NS[t + 1])]
-            if qs[o] == "v":
-                do("v", lambda: g.vector.tensor_copy(out, i), rd, wr)
-            else:
-                do("s", lambda: g.scalar.activation(out, i, AF.Copy), rd, wr)
+            cp(qs[o], "yp%d" % o, (NS[t], NS[t + 1]), "ps%d" % (2 + o), (32, 128))
 
     for t in range(R):
         n = NS[t]
-        wn = "win" if t < 3 else "winf"
-        tb = "tt" if t < 3 else "ttf"
-        sr = "srow" if t < 3 else "srowf"
+        wn, tb = ("win", "ttb") if t < 3 else ("winf", "ttf")
+        sr = "srow%d" % t
         do("s", lambda: g.scalar.activation(T.u64[:, 0:64], T.wc[:, 0:n].indirect(T.fl[:, 0:4]), AF.Copy), [rg("wc", 0, n), rg("fl", 0, 16)], [rg("u64", 0, 64)])
         tt(T.rr[:, 0:P], T.wc[:, 0:n].indirect(T.fl[:, 0:16]), T.mm[:, 0:P], A.mult, [rg("wc", 0, n), rg("fl", 0, 16), rg("mm", 0, P)], [rg("rr", 0, P)])
         tr("t4", 0, "u64", 0, 64)
@@ -294,9 +245,6 @@ def rank_program(g, core, T, topo):
         cp("s", "r8", (2, 4), "r8", (0, 2), (32, 64), (0, 32))
         cp("v", "r8", (4, 8), "r8", (0, 4), (0, 64), (64, 128))
         cp("s", "r8", (4, 8), "r8", (0, 4), (64, 128), (0, 64))
-        if t == 0:
-            slot_row(0)
-            fill("win", 0, 208, 0.0)
         ts(T.off[:, 0:8], T.r8[:, 0:8], 16.0, 16.0, A.mult, A.add, [rg("r8", 0, 8)], [rg("off", 0, 8)])
         do("v", lambda: g.vector.tensor_copy(T[wn][:, 0:512].indirect(T.off[:, 0:8]), T[sr][:, 0:128]), [rg(sr, 0, 128), rg("off", 0, 8)], [rg(wn, 0, 512)])
         tr(tb, 0, wn, 16, 192)
@@ -304,16 +252,13 @@ def rank_program(g, core, T, topo):
         tt(T.a12[:, 0:12], T[tb][:, 0:384:32], T[tb][:, 16:384:32], A.add, [rg(tb, 0, 384)], [rg("a12", 0, 12)])
         tt(T.a6[:, 0:6], T.a12[:, 0:6], T.a12[:, 6:12], A.add, [rg("a12", 0, 12)], [rg("a6", 0, 6)])
         ts(T.lst[:, 0:6], T.a6[:, 0:6], 256.0, None, A.add, None, [rg("a6", 0, 6)], [rg("lst", 0, 6)])
-        wc_, ws_, oc_, os_ = "w%dc" % t, "w%ds" % t, "out%dc" % t, "out%ds" % t
-        do("v", lambda: g.vector.tensor_copy(T[oc_][:, 0:K].bitcast(dt.uint32), T[wc_][:, 0:n].bitcast(dt.uint32).indirect(T.lst[:, 0:6])),
-           [rg(wc_, 0, n), rg("lst", 0, 6)], [rg(oc_, 0, K)])
-        do("s", lambda: g.scalar.activation(T[os_][:, 0:K], T[ws_][:, 0:n].indirect(T.lst[:, 0:6]), AF.Copy),
-           [rg(ws_, 0, n), rg("lst", 0, 6)], [rg(os_, 0, K)])
+        pick("out%d" % t, 0, "w%d" % t, n, "lst", 0, K)
         dst = T.cores[rank ^ PART[t]]
         rid, pid, _ = topo.addr(dst)
         nx = "w%d" % (t + 1)
         l0 = n if t < 3 else 32
-        for k, b in (("c", oc_), ("s", os_)):
+        for k in ("c", "s"):
+            b = "out%d%s" % (t, k)
             i, o = T[b][:, 0:K], T[nx + k][:, l0:l0 + K]
             if k == "c":
                 i, o = i.bitcast(dt.uint8), o.bitcast(dt.uint8)
@@ -325,47 +270,50 @@ def rank_program(g, core, T, topo):
             note("r", "a%s%d" % (k, t), came, [], [rg(nx + k, l0, l0 + K)])
 
         if t == 0:
-            pick_query(1)
+            pick("qr", 128, "q", 128, "qoff", 8, 128)
         if t < 3:
             mm("ps0", "qr", 128 * (t + 1), "w%d" % t, 0, n)
             square("sq", 0, "ps0", 0, n)
-        ts(T.qj[:, 0:8], T.r8[:, 0:8], 0.5, -0.25, A.mult, A.add, [rg("r8", 0, 8)], [rg("qj", 0, 8)])
-        ts(T.e8[:, 0:8], T.r8[:, 0:8], 11.5, None, A.is_lt, None, [rg("r8", 0, 8)], [rg("e8", 0, 8)])
-        tt(T.k8[:, 0:8], T.r8[:, 0:8], T.qj[:, 0:8], A.subtract, [rg("r8", 0, 8), rg("qj", 0, 8)], [rg("k8", 0, 8)])
-        ts(T.n8[:, 0:8], T.k8[:, 0:8], 16.0, float(n), A.mult, A.add, [rg("k8", 0, 8)], [rg("n8", 0, 8)])
-        tt(T.n8[:, 0:8], T.n8[:, 0:8], T.s8[:, 0:8], A.subtract, [rg("n8", 0, 8), rg("s8", 0, 8)], [rg("n8", 0, 8)])
-        tt(T.n8[:, 0:8], T.n8[:, 0:8], T.e8[:, 0:8], A.mult, [rg("n8", 0, 8), rg("e8", 0, 8)], [rg("n8", 0, 8)])
-        tt(T.s8[:, 0:8], T.s8[:, 0:8], T.n8[:, 0:8], A.add, [rg("s8", 0, 8), rg("n8", 0, 8)], [rg("s8", 0, 8)])
-        for a in range(4):
-            run = (8, 2, 4, 2)[a]
-            for c in range(0, 8, run):
-                o = 8 + (c ^ (2 * a))
-                cp("s", "s8", (o, o + run), "s8", (c, c + run), (32 * a, 32 * a + 32))
+        cw, da, db = "cw%d" % t, "dd%d" % (t % 2), "dd%d" % ((t + 1) % 2)
+        for e in range(2):
+            ts(T.offd[:, e:16:2], T.r8[:, 0:8], 16.0, 16.0, A.mult, A.add, [rg("r8", 0, 8)], [rg("offd", 0, 16, 0, 128, e)])
+        tt(T[db][:, 0:P], T[cw][:, 0:512].indirect(T.offd[:, 0:16]), T[da][:, 0:P], A.max, [rg(cw, 0, 512), rg("offd", 0, 16), rg(da, 0, P)], [rg(db, 0, P)])
+        own_list(db)
+        if t == 0:
+            for o in range(O):
+                quantize("wt", 128 * o, 128, "wb")
+                mm("ps%d" % (5 + o), "wt", 128 * o, "w0", 0, P)
         if t < 3:
-            slot_row(t + 1)
+            sn = "srow%d" % (t + 1)
+            tt(T[sn][:, 0:128], T[cw][:, 0:512].indirect(T.off[:, 0:8]), T[sr][:, 0:128], A.max, [rg(cw, 0, 512), rg("off", 0, 8), rg(sr, 0, 128)], [rg(sn, 0, 128)])
             tt(T.wr[:, 0:n], T.wr[:, 0:n], T.sq[:, 0:n], A.add, [rg("wr", 0, n), rg("sq", 0, n)], [rg("wr", 0, n)])
-            ts(T.wc[:, 0:n], T.wr[:, 0:n], EPS, None, A.max, None, [rg("wr", 0, n)], [rg("wc", 0, n)])
+            lift(0, n)
             fill("winf" if t == 2 else "win", 0, 208, 0.0)
-        lists(t < 3, True, t)
         if t > 0:
             new_copies(t - 1, "sss")
+        for h in range(2):
+            for s in range(2):
+                cp("s", "fyf", (8 * h + s, 8 * h + 8, 2), "dt0", (32 * h + 16 * s, P, 64), (0, 32))
+        fy = "fy%d" % t
+        for a in range(4 if t == 3 else 1):
+            ts(T[fy][32 * a:32 * a + 32, 0:16], T.fyf[0:32, 0:16], 256.0, None, A.add, None, [rg("fyf", 0, 16, 0, 32)], [rg(fy, 0, 16, 32 * a, 32 * a + 32)])
+        if t < 3:
+            for a in range(1, 4):
+                dma("y", T[fy][32 * a:32 * a + 32, 0:16], T[fy][0:32, 0:16], [rg(fy, 0, 16, 0, 32)], [rg(fy, 0, 16, 32 * a, 32 * a + 32)])
+        if t == 0:
+            for o in range(O):
+                cp("s", "yp%d" % o, (0, P), "ps%d" % (5 + o), (0, P))
+        else:
             for o in range(O):
                 for h in range(2):
                     y_gather("v" if o == 0 else "s", t - 1, o, h)
             y_store(t - 1, 0, O)
-        if t == 0:
-            for o in range(O):
-                do("v", lambda: g.vector.quantize_mx(T.wtc[:, 128 * o:128 * o + 128], T.wts[:, 128 * o:128 * o + 128], T.wb[:, 512 * o:512 * o + 512]),
-                   [rg("wb", 512 * o, 512 * o + 512)], [rg("wtc", 128 * o, 128 * o + 128), rg("wts", 128 * o, 128 * o + 128)])
-                mm("ps%d" % (5 + o), "wt", 128 * o, "w0", 0, P)
-                out, i = T["yp%d" % o][:, 0:P], T["ps%d" % (5 + o)][:, 0:P]
-                do("s", lambda: g.scalar.activation(out, i, AF.Copy), [rg("ps%d" % (5 + o), 0, 512)], [rg("yp%d" % o, 0, P)])
-            pick_query(2)
-            pick_query(3)
+        if t < 2:
+            pick("qr", 128 * (t + 2), "q", 128, "qoff", 8 * (t + 2), 128)
         if t < 3:
             mm("ps1", "qr", 128 * (t + 1), nx, n - 32, 128)
             square("wr", n, "ps1", 32, K)
-            ts(T.wc[:, n:n + K], T.wr[:, n:n + K], EPS, None, A.max, None, [rg("wr", n, n + K)], [rg("wc", n, n + K)])
+            lift(n, n + K)
             for u in range(t + 2, R):
                 copy_slots(nx, "w%d" % u, n, n + K)
         new_products(t)

@@ -1,4 +1,4 @@
-from concourse.mybir import dt, AluOpType as A, AxisListType, ActivationFunctionType as AF
+from concourse.mybir import dt, AluOpType as A, ActivationFunctionType as AF
 
 P, K, R, O = 256, 96, 4, 3
 PART = [1, 2, 4, 1]
@@ -15,23 +15,23 @@ for _t in range(R):
         SCRATCH[_b + "c"] = ("sbuf", [128, _n], "float8_e4m3fn_x4")
         SCRATCH[_b + "s"] = ("sbuf", [128, _n], "uint8")
     SCRATCH["yb%d" % _t] = ("sbuf", [128, O * P], "float32")
-    SCRATCH["cw%d" % _t] = ("sbuf", [128, 512], "float32")
+    SCRATCH["cw%d" % _t] = ("sbuf", [128, 272], "float32")
     SCRATCH["fy%d" % _t] = ("sbuf", [128, 16], "uint16")
-    SCRATCH["srow%d" % _t] = ("sbuf", [128, 128], "bfloat16" if _t < 3 else "float32")
+    SCRATCH["win%d" % _t] = ("sbuf", [128, 272], "bfloat16" if _t < 3 else "float32")
     SEMAPHORES += ["ac%d" % _t, "as%d" % _t, "lc%d" % _t, "ls%d" % _t]
+for _t in range(R + 1):
+    SCRATCH["srow%d" % _t] = ("sbuf", [128, 160], "bfloat16" if _t < 3 else "float32")
 for _o in range(O):
     SCRATCH["yp%d" % _o] = ("sbuf", [128, NS[4]], "float32")
 for _b in range(8):
     SCRATCH["ps%d" % _b] = ("psum", [128, 512], "float32")
 for _b, _n in (("wr", NS[3]), ("wc", NS[3]), ("sq", 512), ("u64", 64), ("t4", 64), ("rr", P), ("mm", P), ("pr", P), ("p2", 8), ("iot", P),
-               ("c0", 264), ("c1", P), ("dump", 264), ("kk", 8), ("r8", 8), ("winf", 512), ("ttf", 384), ("a12", 16), ("a6", 8), ("s8", 8),
-               ("dd0", P), ("dd1", P), ("dt0", P), ("fyf", 16)):
+               ("ttf", 224), ("tsf", 288), ("a7", 8), ("s8", 8), ("cz", 96), ("ctr", 96)):
     SCRATCH[_b] = ("sbuf", [128, _n], "float32")
-for _b, _n in (("win", 512), ("ttb", 384)):
+for _b, _n in (("ttb", 224), ("tsb", 288), ("c0", P), ("c1", P), ("kk", P), ("r8", 8)):
     SCRATCH[_b] = ("sbuf", [128, _n], "bfloat16")
-for _b, _n in (("qoff", 8 * R), ("off", 8), ("hl", 8), ("offd", 16), ("lst", 8), ("fl", 16)):
+for _b, _n in (("qoff", 8 * R), ("off", 8), ("hl", 8), ("co", 8), ("lst", 16), ("fl", 16)):
     SCRATCH[_b] = ("sbuf", [128, _n], "uint16")
-SCRATCH["qi"] = ("sbuf", [128, 8], "int32")
 
 
 def rank_program(g, core, T, topo):
@@ -128,12 +128,15 @@ def rank_program(g, core, T, topo):
     def tr(ob, o0, ib, i0, n):
         do("v", lambda: g.vector.transpose(T[ob][:, o0:o0 + n], T[ib][:, i0:i0 + n]), [rg(ib, i0, i0 + n)], [rg(ob, o0, o0 + n)])
 
-    def pick(ob, o0, ib, n, lb, l0, k):
-        ol = T[lb][:, l0:l0 + k // 16]
-        c, s, oc, os_ = ib + "c", ib + "s", ob + "c", ob + "s"
-        lr = rg(lb, l0, l0 + k // 16)
-        do("v", lambda: g.vector.tensor_copy(T[oc][:, o0:o0 + k].bitcast(dt.uint32), T[c][:, 0:n].bitcast(dt.uint32).indirect(ol)), [rg(c, 0, n), lr], [rg(oc, o0, o0 + k)])
-        do("s", lambda: g.scalar.activation(T[os_][:, o0:o0 + k], T[s][:, 0:n].indirect(ol), AF.Copy), [rg(s, 0, n), lr], [rg(os_, o0, o0 + k)])
+    def pick_codes(ob, o0, ib, n, lb, l0, k):
+        c, oc = ib + "c", ob + "c"
+        do("v", lambda: g.vector.tensor_copy(T[oc][:, o0:o0 + k].bitcast(dt.uint32), T[c][:, 0:n].bitcast(dt.uint32).indirect(T[lb][:, l0:l0 + k // 16])),
+           [rg(c, 0, n), rg(lb, l0, l0 + k // 16)], [rg(oc, o0, o0 + k)])
+
+    def pick_scales(ob, o0, ib, n, lb, l0, k):
+        s, os_ = ib + "s", ob + "s"
+        do("s", lambda: g.scalar.activation(T[os_][:, o0:o0 + k], T[s][:, 0:n].indirect(T[lb][:, l0:l0 + k // 16]), AF.Copy),
+           [rg(s, 0, n), rg(lb, l0, l0 + k // 16)], [rg(os_, o0, o0 + k)])
 
     def mm(bank, lc, l0, rc, r0, n):
         lh, ls, rh, rs = T[lc + "c"], T[lc + "s"], T[rc + "c"], T[rc + "s"]
@@ -159,49 +162,62 @@ def rank_program(g, core, T, topo):
                 i, o = i.bitcast(dt.uint8), o.bitcast(dt.uint8)
             dma("y", o, i, [rg(a, c0, c1)], [rg(b, c0, c1)])
 
-    def own_list(d):
-        tr("dt0", 0, d, 0, P)
-        ts(T.fl[:, 0:16], T.dt0[:, 0:P:16], 256.0, None, A.add, None, [rg("dt0", 0, P)], [rg("fl", 0, 16)])
+    def turn(t):
+        tb, sr = ("tsb" if t < 3 else "tsf"), "srow%d" % t
+        tr(tb, 0, sr, 16, 128)
+        tr(tb, 128, sr, 0, 160)
+        return tb
 
-    def by_list(out, ob, n, win, lb, k):
-        do("v", lambda: g.vector.tensor_copy(out, T[win][:, 0:P].indirect(T[lb][:, 0:k])), [rg(win, 0, P), rg(lb, 0, k)], [rg(ob, 0, n)])
+    def in_order(out, wr, src, n, k):
+        ts(out, T[src][:, 0:n].indirect(T.co[:, k:k + 1]), 256.0, None, A.add, None, [rg(src, 0, n), rg("co", k, k + 1)], wr)
 
     def iota(b, c0, c1, pattern, base, cm, p0=0, p1=128):
         do("g", lambda: g.iota(T[b][p0:p1, c0:c1], pattern, base, cm, allow_small_or_imprecise_dtypes=True), [], [rg(b, c0, c1, p0, p1)])
 
+    def pads(t):
+        fill("srow%d" % t, 0, 16, 0.0)
+        fill("srow%d" % t, 144, 160, 0.0)
+
     dma("y", T.cb[:], T.c[:], [], [rg("cb", 0, 4 * P)])
     dma("s", T.qb[:, 0:16], T.qt[:, 0:16], [], [rg("qb", 0, 16)])
     dma("y", T.wb[:], T.w[:], [rg("cb", 0, 4 * P)], [rg("wb", 0, 512 * O)])
-    for a in range(4):
-        iota("s8", 0, 8, [[128 * (1 - 2 * (a // 2)), 2], [64 * (1 - 2 * (a % 2)), 2], [1, 2]], 64 * a, 2, 32 * a, 32 * a + 32)
-    iota("iot", 0, P, [[1, P]], -256, 0)
-    iota("p2", 0, 1, [[0, 1]], -256, 2)
-    for t in range(R):
-        iota("cw%d" % t, 16, 208, [[16, 6], [0, 2], [1, 16]], NS[t] - 256, 0)
-        iota("cw%d" % t, 208, 512, [[0, 304]], -1000, 0)
-        iota("cw%d" % t, 0, 16, [[0, 16]], -1000, 0)
-
+    fill("cz", 0, 96, 0.0)
     fill("qb", 16, 512, 0.0)
     for t in range(R):
         fill("qoff", 8 * t, 8 * t + 8, t)
-    fill("c0", 256, 257, -1.0 / 16)
-    fill("win", 0, 208, 0.0)
-    cp("v", "offd", (0, 16, 2), "s8", (0, 8))
-    cp("v", "offd", (1, 16, 2), "s8", (0, 8))
-    cp("v", "hl", (0, 8), "s8", (0, 8))
-    by_list(T.dd0[:, 0:P], "dd0", P, "iot", "offd", 16)
-    own_list("dd0")
+    pads(0)
+    fill("win0", 0, 128, 0.0)
+    fill("cw0", 0, 272, -1000.0)
+    for a in range(4):
+        iota("s8", 0, 8, [[128 * (1 - 2 * (a // 2)), 2], [64 * (1 - 2 * (a % 2)), 2], [1, 2]], 64 * a, 2, 32 * a, 32 * a + 32)
+    iota("cz", 0, 16, [[32, 4], [160, 2], [16, 2]], 0, 0)
+    iota("cz", 16, 32, [[32, 4], [-128, 2], [16, 2]], 128, 0)
+    iota("iot", 0, P, [[1, P]], -256, 0)
+    iota("p2", 0, 1, [[0, 1]], -256, 2)
+    iota("cz", 32, 38, [[1, 3], [4, 2]], 0, 0)
+    iota("cz", 48, 54, [[1, 3], [-3, 2]], 3, 0)
+    iota("cz", 64, 80, [[160, 2], [32, 4], [16, 2]], 0, 0)
+    iota("cz", 80, 96, [[-128, 2], [32, 4], [16, 2]], 128, 0)
+    iota("cw0", 16, 112, [[1, K]], NS[0] - 256, 0)
+
     quantize("q", 0, 128, "qb")
-    pick("qr", 0, "q", 128, "qoff", 0, 128)
-    by_list(T.srow0[:, 0:128], "srow0", 128, "iot", "hl", 8)
+    for t in range(2):
+        pick_codes("qr", 128 * t, "q", 128, "qoff", 8 * t, 128)
+        pick_scales("qr", 128 * t, "q", 128, "qoff", 8 * t, 128)
+    cp("v", "hl", (0, 8), "s8", (0, 8))
+    tr("ctr", 0, "cz", 0, 32)
+    cp("v", "co", (0, 1), "ctr", (0, 1))
+    do("v", lambda: g.vector.tensor_copy(T.srow0[:, 16:144], T.iot[:, 0:P].indirect(T.hl[:, 0:8])), [rg("iot", 0, P), rg("hl", 0, 8)], [rg("srow0", 16, 144)])
+    in_order(T.fl[:, 0:16], [rg("fl", 0, 16)], turn(0), 288, 0)
+    do("s", lambda: g.scalar.activation(T.pr[:, 0:P], T.iot[:, 0:P].indirect(T.fl[:, 0:16]), AF.Copy), [rg("iot", 0, P), rg("fl", 0, 16)], [rg("pr", 0, P)])
     quantize("w0", 0, P, "cb")
     mm("ps0", "qr", 0, "w0", 0, P)
     square("wr", 0, "ps0", 0, P)
-    by_list(T.pr[:, 0:P], "pr", P, "iot", "fl", 16)
     ts(T.mm[:, 0:P], T.pr[:, 0:P], T.p2[:, 0:1], 1.0 - 2.0 ** -24, A.is_gt, A.max, [rg("pr", 0, P), rg("p2", 0, 1)], [rg("mm", 0, P)])
+    tr("ctr", 32, "cz", 32, 64)
     lift(0, P)
-    for t in range(1, R):
-        copy_slots("w0", "w%d" % t, 0, P)
+    copy_slots("w0", "w1", 0, P)
+    copy_slots("w0", "w2", 0, P)
     copy_slots("w0", "w4", 0, 32)
 
     def y_gather(q, t, o, h):
@@ -228,31 +244,37 @@ def rank_program(g, core, T, topo):
 
     for t in range(R):
         n = NS[t]
-        wn, tb = ("win", "ttb") if t < 3 else ("winf", "ttf")
-        sr = "srow%d" % t
+        wn, tb, sr, cw = "win%d" % t, ("ttb" if t < 3 else "ttf"), "srow%d" % t, "cw%d" % t
         do("s", lambda: g.scalar.activation(T.u64[:, 0:64], T.wc[:, 0:n].indirect(T.fl[:, 0:4]), AF.Copy), [rg("wc", 0, n), rg("fl", 0, 16)], [rg("u64", 0, 64)])
+        if t > 0:
+            new_copies(t - 1, "sss")
         tt(T.rr[:, 0:P], T.wc[:, 0:n].indirect(T.fl[:, 0:16]), T.mm[:, 0:P], A.mult, [rg("wc", 0, n), rg("fl", 0, 16), rg("mm", 0, P)], [rg("rr", 0, P)])
         tr("t4", 0, "u64", 0, 64)
-        ts(T.c0[:, 0:P], T.rr[:, 0:P], T.t4[:, 0:1], 1.0 / 16, A.is_lt, A.mult, [rg("rr", 0, P), rg("t4", 0, 1)], [rg("c0", 0, P)])
-        do("s", lambda: g.scalar.activation(T.dump[:, 0:257], T.c0[:, 0:257], AF.Copy, accum_out=T.kk[:, 0:1]), [rg("c0", 0, 257)], [rg("dump", 0, 257), rg("kk", 0, 1)])
-        ts(T.c1[:, 0:P], T.rr[:, 0:P], T.t4[:, 32:33], 1.0 / 16, A.is_lt, A.mult, [rg("rr", 0, P), rg("t4", 32, 33)], [rg("c1", 0, P)])
-        do("v", lambda: g.vector.tensor_reduce(T.kk[:, 1:2], T.c1[:, 0:P], AxisListType.X, A.add), [rg("c1", 0, P)], [rg("kk", 1, 2)])
-        ts(T.qi[:, 0:2], T.kk[:, 0:2], -15.0 / 32, None, A.add, None, [rg("kk", 0, 2)], [rg("qi", 0, 2)])
-        tt(T.r8[:, 0:2], T.kk[:, 0:2], T.qi[:, 0:2], A.add, [rg("kk", 0, 2), rg("qi", 0, 2)], [rg("r8", 0, 2)])
-        cp("v", "r8", (2, 4), "r8", (0, 2), (64, 96), (96, 128))
-        cp("s", "r8", (2, 4), "r8", (0, 2), (0, 32), (32, 64))
-        cp("v", "r8", (2, 4), "r8", (0, 2), (96, 128), (64, 96))
-        cp("s", "r8", (2, 4), "r8", (0, 2), (32, 64), (0, 32))
-        cp("v", "r8", (4, 8), "r8", (0, 4), (0, 64), (64, 128))
-        cp("s", "r8", (4, 8), "r8", (0, 4), (64, 128), (0, 64))
-        ts(T.off[:, 0:8], T.r8[:, 0:8], 16.0, 16.0, A.mult, A.add, [rg("r8", 0, 8)], [rg("off", 0, 8)])
-        do("v", lambda: g.vector.tensor_copy(T[wn][:, 0:512].indirect(T.off[:, 0:8]), T[sr][:, 0:128]), [rg(sr, 0, 128), rg("off", 0, 8)], [rg(wn, 0, 512)])
-        tr(tb, 0, wn, 16, 192)
-        tr(tb, 192, wn, 0, 192)
-        tt(T.a12[:, 0:12], T[tb][:, 0:384:32], T[tb][:, 16:384:32], A.add, [rg(tb, 0, 384)], [rg("a12", 0, 12)])
-        tt(T.a6[:, 0:6], T.a12[:, 0:6], T.a12[:, 6:12], A.add, [rg("a12", 0, 12)], [rg("a6", 0, 6)])
-        ts(T.lst[:, 0:6], T.a6[:, 0:6], 256.0, None, A.add, None, [rg("a6", 0, 6)], [rg("lst", 0, 6)])
-        pick("out%d" % t, 0, "w%d" % t, n, "lst", 0, K)
+        for e in range(2):
+            ts(T["c%d" % e][:, 0:P], T.rr[:, 0:P], T.t4[:, 32 * e:32 * e + 1], None, A.is_lt, None, [rg("rr", 0, P), rg("t4", 32 * e, 32 * e + 1)], [rg("c%d" % e, 0, P)])
+        for e in range(2):
+            do("v", lambda: g.vector.tensor_tensor_scan(T.kk[:, 128 * e:128 * e + 128], T["c%d" % e][:, 0:128], T["c%d" % e][:, 128:256], float(e - 1), A.add, A.add),
+               [rg("c%d" % e, 0, P)], [rg("kk", 128 * e, 128 * e + 128)])
+        cnt = (127, 256, 128)
+        cp("v", "r8", (2, 4), "kk", cnt, (64, 96), (96, 128))
+        cp("s", "r8", (2, 4), "kk", cnt, (0, 32), (32, 64))
+        cp("v", "r8", (2, 4), "kk", cnt, (96, 128), (64, 96))
+        cp("s", "r8", (2, 4), "kk", cnt, (32, 64), (0, 32))
+        cp("v", "r8", (0, 2), "kk", cnt)
+        for o0, o1, i0, i1, c in ((0, 64, 64, 128, 4), (64, 128, 0, 64, 4), (0, 128, 0, 128, 0)):
+            ts(T.off[o0:o1, c:c + 4], T.r8[i0:i1, 0:4], 16.0, None, A.add, None, [rg("r8", 0, 4, i0, i1)], [rg("off", c, c + 4, o0, o1)])
+        if t > 0:
+            for o, h in ((0, 0), (0, 1), (1, 0)):
+                y_gather("s", t - 1, o, h)
+        if t == 0:
+            cp("v", "co", (2, 6, 2), "ctr", (32, 96, 32))
+        do("v", lambda: g.vector.tensor_copy(T[wn][:, 0:272].indirect(T.off[:, 0:8]), T[sr][:, 16:144]), [rg(sr, 16, 144), rg("off", 0, 8)], [rg(wn, 0, 272)])
+        tr(tb, 0, wn, 16, 96)
+        tr(tb, 96, wn, 0, 128)
+        tt(T.a7[:, 0:7], T[tb][:, 0:224:32], T[tb][:, 16:224:32], A.add, [rg(tb, 0, 224)], [rg("a7", 0, 7)])
+        in_order(T.lst[:, 0:16], [rg("lst", 0, 16)], "a7", 7, 2)
+        pick_codes("out%d" % t, 0, "w%d" % t, n, "lst", 0, K)
+        pick_scales("out%d" % t, 0, "w%d" % t, n, "lst", 0, K)
         dst = T.cores[rank ^ PART[t]]
         rid, pid, _ = topo.addr(dst)
         nx = "w%d" % (t + 1)
@@ -269,53 +291,58 @@ def rank_program(g, core, T, topo):
             count["a%s%d" % (k, t)] = came
             note("r", "a%s%d" % (k, t), came, [], [rg(nx + k, l0, l0 + K)])
 
-        if t == 0:
-            pick("qr", 128, "q", 128, "qoff", 8, 128)
         if t < 3:
             mm("ps0", "qr", 128 * (t + 1), "w%d" % t, 0, n)
             square("sq", 0, "ps0", 0, n)
-        cw, da, db = "cw%d" % t, "dd%d" % (t % 2), "dd%d" % ((t + 1) % 2)
-        for e in range(2):
-            ts(T.offd[:, e:16:2], T.r8[:, 0:8], 16.0, 16.0, A.mult, A.add, [rg("r8", 0, 8)], [rg("offd", 0, 16, 0, 128, e)])
-        tt(T[db][:, 0:P], T[cw][:, 0:512].indirect(T.offd[:, 0:16]), T[da][:, 0:P], A.max, [rg(cw, 0, 512), rg("offd", 0, 16), rg(da, 0, P)], [rg(db, 0, P)])
-        own_list(db)
+        sn = "srow%d" % (t + 1)
+        if t == 0:
+            pads(1)
+            for u in range(1, R):
+                iota("cw%d" % u, 0, 272, [[0, 272]], -1000, 0)
+                iota("cw%d" % u, 16, 112, [[1, K]], NS[u] - 256, 0)
+                iota("win%d" % u, 0, 128, [[0, 128]], 0, 0)
+                for c in (0, 144):
+                    iota("srow%d" % (u + 1), c, c + 16, [[0, 16]], 0, 0)
+        tt(T[sn][:, 16:144], T[cw][:, 0:272].indirect(T.off[:, 0:8]), T[sr][:, 16:144], A.max, [rg(cw, 0, 272), rg("off", 0, 8), rg(sr, 16, 144)], [rg(sn, 16, 144)])
+        tw = turn(t + 1)
+        if t < 3:
+            in_order(T.fl[:, 0:16], [rg("fl", 0, 16)], tw, 288, 0)
+        fy = "fy%d" % t
+        in_order(T[fy][:, 0:16], [rg(fy, 0, 16)], tw, 288, 4)
+        if t < 3:
+            for a in range(1, 4):
+                dma("y", T[fy][32 * a:32 * a + 32, 0:16], T[fy][0:32, 0:16], [rg(fy, 0, 16, 0, 32)], [rg(fy, 0, 16, 32 * a, 32 * a + 32)])
+            tt(T.wr[:, 0:n], T.wr[:, 0:n], T.sq[:, 0:n], A.add, [rg("wr", 0, n), rg("sq", 0, n)], [rg("wr", 0, n)])
+            lift(0, n)
+        else:
+            for a in range(1, 4):
+                cp("v", fy, (0, 16), fy, (0, 16), (32 * a, 32 * a + 32), (0, 32))
         if t == 0:
             for o in range(O):
                 quantize("wt", 128 * o, 128, "wb")
                 mm("ps%d" % (5 + o), "wt", 128 * o, "w0", 0, P)
-        if t < 3:
-            sn = "srow%d" % (t + 1)
-            tt(T[sn][:, 0:128], T[cw][:, 0:512].indirect(T.off[:, 0:8]), T[sr][:, 0:128], A.max, [rg(cw, 0, 512), rg("off", 0, 8), rg(sr, 0, 128)], [rg(sn, 0, 128)])
-            tt(T.wr[:, 0:n], T.wr[:, 0:n], T.sq[:, 0:n], A.add, [rg("wr", 0, n), rg("sq", 0, n)], [rg("wr", 0, n)])
-            lift(0, n)
-            fill("winf" if t == 2 else "win", 0, 208, 0.0)
-        if t > 0:
-            new_copies(t - 1, "sss")
-        for h in range(2):
-            for s in range(2):
-                cp("s", "fyf", (8 * h + s, 8 * h + 8, 2), "dt0", (32 * h + 16 * s, P, 64), (0, 32))
-        fy = "fy%d" % t
-        for a in range(4 if t == 3 else 1):
-            ts(T[fy][32 * a:32 * a + 32, 0:16], T.fyf[0:32, 0:16], 256.0, None, A.add, None, [rg("fyf", 0, 16, 0, 32)], [rg(fy, 0, 16, 32 * a, 32 * a + 32)])
-        if t < 3:
-            for a in range(1, 4):
-                dma("y", T[fy][32 * a:32 * a + 32, 0:16], T[fy][0:32, 0:16], [rg(fy, 0, 16, 0, 32)], [rg(fy, 0, 16, 32 * a, 32 * a + 32)])
-        if t == 0:
+            for u in range(2, R):
+                pick_codes("qr", 128 * u, "q", 128, "qoff", 8 * u, 128)
+                pick_scales("qr", 128 * u, "q", 128, "qoff", 8 * u, 128)
             for o in range(O):
                 cp("s", "yp%d" % o, (0, P), "ps%d" % (5 + o), (0, P))
         else:
-            for o in range(O):
-                for h in range(2):
-                    y_gather("v" if o == 0 else "s", t - 1, o, h)
-            y_store(t - 1, 0, O)
-        if t < 2:
-            pick("qr", 128 * (t + 2), "q", 128, "qoff", 8 * (t + 2), 128)
+            if t == 3:
+                y_store(2, 0, 1)
+            for o, h in ((1, 1), (2, 0), (2, 1)):
+                y_gather("s", t - 1, o, h)
+            if t == 3:
+                y_store(2, 1, 3)
         if t < 3:
             mm("ps1", "qr", 128 * (t + 1), nx, n - 32, 128)
             square("wr", n, "ps1", 32, K)
             lift(n, n + K)
             for u in range(t + 2, R):
                 copy_slots(nx, "w%d" % u, n, n + K)
+            if t == 0:
+                copy_slots("w0", "w3", 0, P)
+            else:
+                y_store(t - 1, 0, O)
         new_products(t)
     new_copies(3, "svs")
     for o in range(O):

@@ -6,18 +6,18 @@ NS = [P + K * t for t in range(R + 1)]
 EPS = 2.0 ** -125
 
 SCRATCH = {"cb": ("sbuf", [128, 4 * P], "bfloat16"), "qb": ("sbuf", [128, 512], "bfloat16"), "wb": ("sbuf", [128, 512 * O], "bfloat16")}
-SEMAPHORES = ["sg", "sv", "ss", "st"] + ["d%d" % i for i in range(48)]
-for _b, _n in (("q", 128), ("qr", 128 * R), ("wt", 128 * O), ("w4", 128)):
+SEMAPHORES = ["sg", "sv", "ss", "st", "al", "ll"] + ["d%d" % i for i in range(48)]
+for _b, _n in (("q", 128), ("qr", 128 * R), ("wt", 128 * O), ("w4", 128), ("h", P), ("out1", K), ("out2", K), ("out3", K)):
     SCRATCH[_b + "c"] = ("sbuf", [128, _n], "float8_e4m3fn_x4")
     SCRATCH[_b + "s"] = ("sbuf", [128, _n], "uint8")
 for _t in range(R):
-    for _b, _n in (("w%d" % _t, NS[_t]), ("out%d" % _t, K)):
-        SCRATCH[_b + "c"] = ("sbuf", [128, _n], "float8_e4m3fn_x4")
-        SCRATCH[_b + "s"] = ("sbuf", [128, _n], "uint8")
+    SCRATCH["w%dc" % _t] = ("sbuf", [128, NS[_t]], "float8_e4m3fn_x4")
+    SCRATCH["w%ds" % _t] = ("sbuf", [128, NS[_t]], "uint8")
     SCRATCH["yb%d" % _t] = ("sbuf", [128, O * P], "float32")
     SCRATCH["cw%d" % _t] = ("sbuf", [128, 272], "float32")
     SCRATCH["fy%d" % _t] = ("sbuf", [128, 16], "uint16")
     SCRATCH["win%d" % _t] = ("sbuf", [128, 272], "bfloat16" if _t < 3 else "float32")
+    SCRATCH["lst%d" % _t] = ("sbuf", [128, 16], "uint16")
     SEMAPHORES += ["ac%d" % _t, "as%d" % _t, "lc%d" % _t, "ls%d" % _t]
 for _t in range(R + 1):
     SCRATCH["srow%d" % _t] = ("sbuf", [128, 160], "bfloat16" if _t < 3 else "float32")
@@ -25,12 +25,12 @@ for _o in range(O):
     SCRATCH["yp%d" % _o] = ("sbuf", [128, NS[4]], "float32")
 for _b in range(8):
     SCRATCH["ps%d" % _b] = ("psum", [128, 512], "float32")
-for _b, _n in (("wr", NS[3]), ("wc", NS[3]), ("sq", 512), ("u64", 64), ("t4", 64), ("rr", P), ("mm", P), ("pr", P), ("p2", 8), ("iot", P),
+for _b, _n in (("wr", NS[3]), ("wc", NS[3]), ("sq", 512), ("hq", P), ("u64", 64), ("t4", 64), ("rr", P), ("mm", P), ("pr", P), ("p2", 8), ("iot", P),
                ("ttf", 224), ("tsf", 288), ("a7", 8), ("s8", 8), ("cz", 96), ("ctr", 96)):
     SCRATCH[_b] = ("sbuf", [128, _n], "float32")
 for _b, _n in (("ttb", 224), ("tsb", 288), ("c0", P), ("c1", P), ("kk", P), ("r8", 8)):
     SCRATCH[_b] = ("sbuf", [128, _n], "bfloat16")
-for _b, _n in (("qoff", 8 * R), ("off", 8), ("hl", 8), ("co", 8), ("lst", 16), ("fl", 16)):
+for _b, _n in (("qoff", 8 * R), ("off", 8), ("hl", 8), ("co", 8), ("fl", 16), ("alst", 8)):
     SCRATCH[_b] = ("sbuf", [128, _n], "uint16")
 
 
@@ -101,6 +101,22 @@ def rank_program(g, core, T, topo):
         Q[q].dma_start(out, in_).then_inc(T.sem[sem], 16)
         count[sem] = 16
         note("y" if q == "y" else q + "d", sem, 16, reads, writes)
+
+    def send(t, out, in_, reads, writes, sa, sl):
+        dst = T.cores[rank ^ PART[t]]
+        rid, pid, _ = topo.addr(dst)
+        need("g", reads, [])
+        g.remote_dma(out, in_, T.sem[sa], T.sem[sl], pid, rid, topo.mask(core, dst))
+        count[sl] = len(topo.engines(core, dst))
+        count[sa] = len(topo.engines(dst, core))
+        note("r", sa, count[sa], [], writes)
+
+    def send_codes(t, ob, o0, ib, n):
+        for k in ("c", "s"):
+            i, o = T[ib + k][:, 0:n], T[ob + k][:, o0:o0 + n]
+            if k == "c":
+                i, o = i.bitcast(dt.uint8), o.bitcast(dt.uint8)
+            send(t, o, i, [rg(ib + k, 0, n)], [rg(ob + k, o0, o0 + n)], "a%s%d" % (k, t), "l%s%d" % (k, t))
 
     def cp(q, ob, oc, ib, ic, p=(0, 128), ip=None):
         ip = ip or p
@@ -174,51 +190,60 @@ def rank_program(g, core, T, topo):
     def iota(b, c0, c1, pattern, base, cm, p0=0, p1=128):
         do("g", lambda: g.iota(T[b][p0:p1, c0:c1], pattern, base, cm, allow_small_or_imprecise_dtypes=True), [], [rg(b, c0, c1, p0, p1)])
 
-    def pads(t):
-        fill("srow%d" % t, 0, 16, 0.0)
-        fill("srow%d" % t, 144, 160, 0.0)
+    def g_tables(u):
+        iota("cw%d" % u, 0, 272, [[0, 272]], -1000, 0)
+        iota("cw%d" % u, 16, 112, [[1, K]], NS[u] - 256, 0)
+        iota("win%d" % u, 0, 128, [[0, 128]], 0, 0)
 
-    dma("y", T.cb[:], T.c[:], [], [rg("cb", 0, 4 * P)])
+    def g_pads(u):
+        for c in (0, 144):
+            iota("srow%d" % u, c, c + 16, [[0, 16]], 0, 0)
+
+    for h in range(2):
+        dma("y", T.cb[:, 2 * P * h:2 * P * h + 2 * P], T.c[:, 2 * P * h:2 * P * h + 2 * P], [], [rg("cb", 2 * P * h, 2 * P * h + 2 * P)])
     dma("s", T.qb[:, 0:16], T.qt[:, 0:16], [], [rg("qb", 0, 16)])
     dma("y", T.wb[:], T.w[:], [rg("cb", 0, 4 * P)], [rg("wb", 0, 512 * O)])
     fill("cz", 0, 96, 0.0)
     fill("qb", 16, 512, 0.0)
     for t in range(R):
         fill("qoff", 8 * t, 8 * t + 8, t)
-    pads(0)
+    fill("srow0", 0, 16, 0.0)
+    fill("srow0", 144, 160, 0.0)
     fill("win0", 0, 128, 0.0)
     fill("cw0", 0, 272, -1000.0)
     for a in range(4):
         iota("s8", 0, 8, [[128 * (1 - 2 * (a // 2)), 2], [64 * (1 - 2 * (a % 2)), 2], [1, 2]], 64 * a, 2, 32 * a, 32 * a + 32)
+    iota("iot", 0, P, [[1, P]], -256, 0)
     iota("cz", 0, 16, [[32, 4], [160, 2], [16, 2]], 0, 0)
     iota("cz", 16, 32, [[32, 4], [-128, 2], [16, 2]], 128, 0)
-    iota("iot", 0, P, [[1, P]], -256, 0)
     iota("p2", 0, 1, [[0, 1]], -256, 2)
+
+    quantize("q", 0, 128, "qb")
+    for t in range(R):
+        pick_scales("qr", 128 * t, "q", 128, "qoff", 8 * t, 128)
+    pick_codes("qr", 0, "q", 128, "qoff", 0, 128)
+    cp("v", "hl", (0, 8), "s8", (0, 8))
+    do("v", lambda: g.vector.tensor_copy(T.srow0[:, 16:144], T.iot[:, 0:P].indirect(T.hl[:, 0:8])), [rg("iot", 0, P), rg("hl", 0, 8)], [rg("srow0", 16, 144)])
+    tw = turn(0)
+    tr("ctr", 0, "cz", 0, 32)
+    cp("v", "co", (0, 1), "ctr", (0, 1))
+    in_order(T.fl[:, 0:16], [rg("fl", 0, 16)], tw, 288, 0)
+    do("s", lambda: g.scalar.activation(T.pr[:, 0:P], T.iot[:, 0:P].indirect(T.fl[:, 0:16]), AF.Copy), [rg("iot", 0, P), rg("fl", 0, 16)], [rg("pr", 0, P)])
+    for h in range(2):
+        quantize("w0", 128 * h, 128, "cb")
+        mm("ps%d" % h, "qr", 0, "w0", 128 * h, 128)
+        square("wr", 128 * h, "ps%d" % h, 0, 128)
+    send_codes(0, "h", 0, "w0", P)
     iota("cz", 32, 38, [[1, 3], [4, 2]], 0, 0)
     iota("cz", 48, 54, [[1, 3], [-3, 2]], 3, 0)
     iota("cz", 64, 80, [[160, 2], [32, 4], [16, 2]], 0, 0)
     iota("cz", 80, 96, [[-128, 2], [32, 4], [16, 2]], 128, 0)
     iota("cw0", 16, 112, [[1, K]], NS[0] - 256, 0)
-
-    quantize("q", 0, 128, "qb")
-    for t in range(2):
-        pick_codes("qr", 128 * t, "q", 128, "qoff", 8 * t, 128)
-        pick_scales("qr", 128 * t, "q", 128, "qoff", 8 * t, 128)
-    cp("v", "hl", (0, 8), "s8", (0, 8))
-    tr("ctr", 0, "cz", 0, 32)
-    cp("v", "co", (0, 1), "ctr", (0, 1))
-    do("v", lambda: g.vector.tensor_copy(T.srow0[:, 16:144], T.iot[:, 0:P].indirect(T.hl[:, 0:8])), [rg("iot", 0, P), rg("hl", 0, 8)], [rg("srow0", 16, 144)])
-    in_order(T.fl[:, 0:16], [rg("fl", 0, 16)], turn(0), 288, 0)
-    do("s", lambda: g.scalar.activation(T.pr[:, 0:P], T.iot[:, 0:P].indirect(T.fl[:, 0:16]), AF.Copy), [rg("iot", 0, P), rg("fl", 0, 16)], [rg("pr", 0, P)])
-    quantize("w0", 0, P, "cb")
-    mm("ps0", "qr", 0, "w0", 0, P)
-    square("wr", 0, "ps0", 0, P)
+    g_pads(1)
+    pick_codes("qr", 128, "q", 128, "qoff", 8, 128)
     ts(T.mm[:, 0:P], T.pr[:, 0:P], T.p2[:, 0:1], 1.0 - 2.0 ** -24, A.is_gt, A.max, [rg("pr", 0, P), rg("p2", 0, 1)], [rg("mm", 0, P)])
-    tr("ctr", 32, "cz", 32, 64)
-    lift(0, P)
-    copy_slots("w0", "w1", 0, P)
-    copy_slots("w0", "w2", 0, P)
-    copy_slots("w0", "w4", 0, 32)
+    for h in range(2):
+        lift(128 * h, 128 * h + 128)
 
     def y_gather(q, t, o, h):
         n = NS[t + 1]
@@ -238,16 +263,19 @@ def rank_program(g, core, T, topo):
         for o in range(O):
             mm("ps%d" % (2 + o), "wt", 128 * o, "w%d" % (t + 1), NS[t] - 32 if t < 3 else 0, 128)
 
-    def new_copies(t, qs):
-        for o in range(O):
-            cp(qs[o], "yp%d" % o, (NS[t], NS[t + 1]), "ps%d" % (2 + o), (32, 128))
+    def new_copy(t, q, o):
+        cp(q, "yp%d" % o, (NS[t], NS[t + 1]), "ps%d" % (2 + o), (32, 128))
 
     for t in range(R):
         n = NS[t]
-        wn, tb, sr, cw = "win%d" % t, ("ttb" if t < 3 else "ttf"), "srow%d" % t, "cw%d" % t
+        wn, tb, sr, cw, ls = "win%d" % t, ("ttb" if t < 3 else "ttf"), "srow%d" % t, "cw%d" % t, "lst%d" % t
         do("s", lambda: g.scalar.activation(T.u64[:, 0:64], T.wc[:, 0:n].indirect(T.fl[:, 0:4]), AF.Copy), [rg("wc", 0, n), rg("fl", 0, 16)], [rg("u64", 0, 64)])
-        if t > 0:
-            new_copies(t - 1, "sss")
+        if t == 1:
+            for o in range(O):
+                cp("s", "yp%d" % o, (0, P), "ps%d" % (5 + o), (0, P))
+        elif t > 1:
+            for o in range(O):
+                new_copy(t - 1, "s", o)
         tt(T.rr[:, 0:P], T.wc[:, 0:n].indirect(T.fl[:, 0:16]), T.mm[:, 0:P], A.mult, [rg("wc", 0, n), rg("fl", 0, 16), rg("mm", 0, P)], [rg("rr", 0, P)])
         tr("t4", 0, "u64", 0, 64)
         for e in range(2):
@@ -261,48 +289,42 @@ def rank_program(g, core, T, topo):
         cp("v", "r8", (2, 4), "kk", cnt, (96, 128), (64, 96))
         cp("s", "r8", (2, 4), "kk", cnt, (32, 64), (0, 32))
         cp("v", "r8", (0, 2), "kk", cnt)
+        if t == 0:
+            tr("ctr", 32, "cz", 32, 64)
         for o0, o1, i0, i1, c in ((0, 64, 64, 128, 4), (64, 128, 0, 64, 4), (0, 128, 0, 128, 0)):
             ts(T.off[o0:o1, c:c + 4], T.r8[i0:i1, 0:4], 16.0, None, A.add, None, [rg("r8", 0, 4, i0, i1)], [rg("off", c, c + 4, o0, o1)])
-        if t > 0:
-            for o, h in ((0, 0), (0, 1), (1, 0)):
-                y_gather("s", t - 1, o, h)
+        if t == 1:
+            for o in range(O):
+                new_copy(0, "s", o)
+        for o, h in (((0, 0),) if t == 1 else ((0, 0), (0, 1), (1, 0)) if t > 1 else ()):
+            y_gather("s", t - 1, o, h)
         if t == 0:
             cp("v", "co", (2, 6, 2), "ctr", (32, 96, 32))
         do("v", lambda: g.vector.tensor_copy(T[wn][:, 0:272].indirect(T.off[:, 0:8]), T[sr][:, 16:144]), [rg(sr, 16, 144), rg("off", 0, 8)], [rg(wn, 0, 272)])
         tr(tb, 0, wn, 16, 96)
         tr(tb, 96, wn, 0, 128)
         tt(T.a7[:, 0:7], T[tb][:, 0:224:32], T[tb][:, 16:224:32], A.add, [rg(tb, 0, 224)], [rg("a7", 0, 7)])
-        in_order(T.lst[:, 0:16], [rg("lst", 0, 16)], "a7", 7, 2)
-        pick_codes("out%d" % t, 0, "w%d" % t, n, "lst", 0, K)
-        pick_scales("out%d" % t, 0, "w%d" % t, n, "lst", 0, K)
-        dst = T.cores[rank ^ PART[t]]
-        rid, pid, _ = topo.addr(dst)
+        in_order(T[ls][:, 0:16], [rg(ls, 0, 16)], "a7", 7, 2)
         nx = "w%d" % (t + 1)
-        l0 = n if t < 3 else 32
-        for k in ("c", "s"):
-            b = "out%d%s" % (t, k)
-            i, o = T[b][:, 0:K], T[nx + k][:, l0:l0 + K]
-            if k == "c":
-                i, o = i.bitcast(dt.uint8), o.bitcast(dt.uint8)
-            need("g", [rg(b, 0, K)], [])
-            g.remote_dma(o, i, T.sem["a%s%d" % (k, t)], T.sem["l%s%d" % (k, t)], pid, rid, topo.mask(core, dst))
-            came = len(topo.engines(dst, core))
-            count["l%s%d" % (k, t)] = len(topo.engines(core, dst))
-            count["a%s%d" % (k, t)] = came
-            note("r", "a%s%d" % (k, t), came, [], [rg(nx + k, l0, l0 + K)])
+        if t == 0:
+            send(0, T.alst[:, 0:6], T.lst0[:, 0:6], [rg("lst0", 0, 6)], [rg("alst", 0, 6)], "al", "ll")
+        else:
+            pick_codes("out%d" % t, 0, "w%d" % t, n, ls, 0, K)
+            pick_scales("out%d" % t, 0, "w%d" % t, n, ls, 0, K)
+            send_codes(t, nx, n if t < 3 else 32, "out%d" % t, K)
 
+        if t == 1:
+            pick_codes("qr", 256, "q", 128, "qoff", 16, 128)
         if t < 3:
             mm("ps0", "qr", 128 * (t + 1), "w%d" % t, 0, n)
             square("sq", 0, "ps0", 0, n)
-        sn = "srow%d" % (t + 1)
         if t == 0:
-            pads(1)
-            for u in range(1, R):
-                iota("cw%d" % u, 0, 272, [[0, 272]], -1000, 0)
-                iota("cw%d" % u, 16, 112, [[1, K]], NS[u] - 256, 0)
-                iota("win%d" % u, 0, 128, [[0, 128]], 0, 0)
-                for c in (0, 144):
-                    iota("srow%d" % (u + 1), c, c + 16, [[0, 16]], 0, 0)
+            mm("ps1", "qr", 128, "h", 0, P)
+            square("hq", 0, "ps1", 0, P)
+        if t < 3:
+            g_tables(t + 1)
+            g_pads(t + 2)
+        sn = "srow%d" % (t + 1)
         tt(T[sn][:, 16:144], T[cw][:, 0:272].indirect(T.off[:, 0:8]), T[sr][:, 16:144], A.max, [rg(cw, 0, 272), rg("off", 0, 8), rg(sr, 16, 144)], [rg(sn, 16, 144)])
         tw = turn(t + 1)
         if t < 3:
@@ -321,11 +343,12 @@ def rank_program(g, core, T, topo):
             for o in range(O):
                 quantize("wt", 128 * o, 128, "wb")
                 mm("ps%d" % (5 + o), "wt", 128 * o, "w0", 0, P)
-            for u in range(2, R):
-                pick_codes("qr", 128 * u, "q", 128, "qoff", 8 * u, 128)
-                pick_scales("qr", 128 * u, "q", 128, "qoff", 8 * u, 128)
-            for o in range(O):
-                cp("s", "yp%d" % o, (0, P), "ps%d" % (5 + o), (0, P))
+            copy_slots("w0", "w1", 0, P)
+            copy_slots("w0", "w4", 0, 32)
+        elif t == 1:
+            pick_codes("qr", 384, "q", 128, "qoff", 24, 128)
+            for o, h in ((0, 1), (1, 0), (1, 1), (2, 0), (2, 1)):
+                y_gather("s", 0, o, h)
         else:
             if t == 3:
                 y_store(2, 0, 1)
@@ -334,20 +357,32 @@ def rank_program(g, core, T, topo):
             if t == 3:
                 y_store(2, 1, 3)
         if t < 3:
-            mm("ps1", "qr", 128 * (t + 1), nx, n - 32, 128)
-            square("wr", n, "ps1", 32, K)
+            if t == 0:
+                do("s", lambda: g.scalar.activation(T.wr[:, n:n + K], T.hq[:, 0:P].indirect(T.alst[:, 0:6]), AF.Copy), [rg("hq", 0, P), rg("alst", 0, 6)], [rg("wr", n, n + K)])
+                pick_codes("w1", n, "h", P, "alst", 0, K)
+                pick_scales("w1", n, "h", P, "alst", 0, K)
+            else:
+                mm("ps1", "qr", 128 * (t + 1), nx, n - 32, 128)
+                square("wr", n, "ps1", 32, K)
             lift(n, n + K)
+            if t == 0:
+                for u in range(2, R):
+                    copy_slots("w0", "w%d" % u, 0, P)
             for u in range(t + 2, R):
                 copy_slots(nx, "w%d" % u, n, n + K)
-            if t == 0:
-                copy_slots("w0", "w3", 0, P)
-            else:
+            if t > 0:
                 y_store(t - 1, 0, O)
         new_products(t)
-    new_copies(3, "svs")
+    new_copy(3, "s", 0)
+    y_gather("s", 3, 0, 0)
+    y_gather("v", 3, 0, 1)
+    new_copy(3, "v", 1)
+    new_copy(3, "s", 2)
+    y_gather("v", 3, 1, 0)
+    y_gather("s", 3, 1, 1)
+    y_gather("v", 3, 2, 0)
+    y_gather("s", 3, 2, 1)
     for o in range(O):
-        y_gather("v", 3, o, 0)
-        y_gather("s", 3, o, 1)
         y_store(3, o, o + 1)
 
     for sem in count:

from concourse.mybir import dt, AluOpType as A, ActivationFunctionType as AF

P, K, R, O = 256, 96, 4, 3
PART = [1, 2, 4, 1]
NS = [P + K * t for t in range(R + 1)]
EPS = 2.0 ** -125

SCRATCH = {"cb": ("sbuf", [128, 4 * P], "bfloat16"), "qb": ("sbuf", [128, 512], "bfloat16"), "wb": ("sbuf", [128, 512 * O], "bfloat16")}
SEMAPHORES = ["sg", "sv", "ss", "st", "al", "ll"] + ["d%d" % i for i in range(48)]
for _b, _n in (("q", 128), ("qr", 128 * R), ("wt", 128 * O), ("w4", 128), ("h", P), ("out1", K), ("out2", K), ("out3", K)):
    SCRATCH[_b + "c"] = ("sbuf", [128, _n], "float8_e4m3fn_x4")
    SCRATCH[_b + "s"] = ("sbuf", [128, _n], "uint8")
for _t in range(R):
    SCRATCH["w%dc" % _t] = ("sbuf", [128, NS[_t]], "float8_e4m3fn_x4")
    SCRATCH["w%ds" % _t] = ("sbuf", [128, NS[_t]], "uint8")
    SCRATCH["yb%d" % _t] = ("sbuf", [128, O * P], "float32")
    SCRATCH["cw%d" % _t] = ("sbuf", [128, 272], "float32")
    SCRATCH["fy%d" % _t] = ("sbuf", [128, 16], "uint16")
    SCRATCH["win%d" % _t] = ("sbuf", [128, 272], "bfloat16" if _t < 3 else "float32")
    SCRATCH["lst%d" % _t] = ("sbuf", [128, 16], "uint16")
    SEMAPHORES += ["ac%d" % _t, "as%d" % _t, "lc%d" % _t, "ls%d" % _t]
for _t in range(R + 1):
    SCRATCH["srow%d" % _t] = ("sbuf", [128, 160], "bfloat16" if _t < 3 else "float32")
for _o in range(O):
    SCRATCH["yp%d" % _o] = ("sbuf", [128, NS[4]], "float32")
for _b in range(8):
    SCRATCH["ps%d" % _b] = ("psum", [128, 512], "float32")
for _b, _n in (("wr", NS[3]), ("wc", NS[3]), ("sq", 512), ("hq", P), ("u64", 64), ("t4", 64), ("rr", P), ("mm", P), ("pr", P), ("p2", 8), ("iot", P),
               ("ttf", 224), ("tsf", 288), ("a7", 8), ("s8", 8), ("cz", 96), ("ctr", 96)):
    SCRATCH[_b] = ("sbuf", [128, _n], "float32")
for _b, _n in (("ttb", 224), ("tsb", 288), ("c0", P), ("c1", P), ("kk", P), ("r8", 8)):
    SCRATCH[_b] = ("sbuf", [128, _n], "bfloat16")
for _b, _n in (("qoff", 8 * R), ("off", 8), ("hl", 8), ("co", 8), ("fl", 16), ("alst", 8)):
    SCRATCH[_b] = ("sbuf", [128, _n], "uint16")


def rank_program(g, core, T, topo):
    rank = T.rank_of(core)
    if rank is None:
        return
    Q = {"g": g, "v": g.vector, "s": g.scalar, "t": g.tensor, "y": g.sync}
    own = {"g": "sg", "v": "sv", "s": "ss", "t": "st"}
    count = {}
    waited = {q: {} for q in Q}
    recs = {}
    ndma = [0]

    def rg(b, c0, c1, p0=0, p1=128, lane=None):
        return (b, c0, c1, p0, p1, lane)

    def meets(a, b):
        if a[0][:2] == "ps":
            return True
        if a[5] is not None and b[5] is not None and a[5] != b[5]:
            return False
        return a[1] < b[2] and b[1] < a[2] and a[3] < b[4] and b[3] < a[4]

    def covers(a, b):
        return a[0][:2] == "ps" or (a[5] is None and a[1] <= b[1] and a[2] >= b[2] and a[3] <= b[3] and a[4] >= b[4])

    def need(q, reads, writes):
        w = {}
        for regs, wr in ((reads, False), (writes, True)):
            for r in regs:
                for (x, xq, sem, n, xw) in recs.get(r[0], []):
                    if not (wr or xw) or not meets(r, x):
                        continue
                    if wr and not xw and xq == q and q != "y":
                        continue
                    if r[0][:2] == "ps" and xq == q:
                        continue
                    w[sem] = max(w.get(sem, 0), n)
        for sem in w:
            if waited[q].get(sem, 0) < w[sem]:
                Q[q].wait_ge(T.sem[sem], w[sem])
                waited[q][sem] = w[sem]

    def note(q, sem, n, reads, writes):
        for r in writes:
            recs[r[0]] = [e for e in recs.get(r[0], []) if not covers(r, e[0])]
        for r in writes:
            recs.setdefault(r[0], []).append((r, q, sem, n, True))
        for r in reads:
            recs.setdefault(r[0], []).append((r, q, sem, n, False))

    def do(q, call, reads, writes):
        need(q, reads, writes)
        if q == "g" and count.get("sg", 0) > waited["g"].get("sg", 0):
            g.wait_ge(T.sem.sg, count["sg"])
            waited["g"]["sg"] = count["sg"]
        ins = call()
        sem = own[q]
        count[sem] = count.get(sem, 0) + 1
        ins.then_inc(T.sem[sem], 1)
        note(q, sem, count[sem], reads, writes)

    def dma(q, out, in_, reads, writes):
        need(q, reads, writes)
        sem = "d%d" % ndma[0]
        ndma[0] += 1
        Q[q].dma_start(out, in_).then_inc(T.sem[sem], 16)
        count[sem] = 16
        note("y" if q == "y" else q + "d", sem, 16, reads, writes)

    def send(t, out, in_, reads, writes, sa, sl):
        dst = T.cores[rank ^ PART[t]]
        rid, pid, _ = topo.addr(dst)
        need("g", reads, [])
        g.remote_dma(out, in_, T.sem[sa], T.sem[sl], pid, rid, topo.mask(core, dst))
        count[sl] = len(topo.engines(core, dst))
        count[sa] = len(topo.engines(dst, core))
        note("r", sa, count[sa], [], writes)

    def send_codes(t, ob, o0, ib, n):
        for k in ("c", "s"):
            i, o = T[ib + k][:, 0:n], T[ob + k][:, o0:o0 + n]
            if k == "c":
                i, o = i.bitcast(dt.uint8), o.bitcast(dt.uint8)
            send(t, o, i, [rg(ib + k, 0, n)], [rg(ob + k, o0, o0 + n)], "a%s%d" % (k, t), "l%s%d" % (k, t))

    def cp(q, ob, oc, ib, ic, p=(0, 128), ip=None):
        ip = ip or p
        o = T[ob][p[0]:p[1], slice(*oc)]
        i = T[ib][ip[0]:ip[1], slice(*ic)]
        rd = [rg(ib, ic[0], ic[1], ip[0], ip[1])]
        wr = [rg(ob, oc[0], oc[1], p[0], p[1], (oc[0] % oc[2]) if len(oc) > 2 else None)]
        if q == "v":
            do("v", lambda: g.vector.tensor_copy(o, i), rd, wr)
        else:
            do("s", lambda: g.scalar.activation(o, i, AF.Copy), rd, wr)

    def ts(out, in0, s1, s2, op0, op1, rd, wr):
        if op1 is None:
            do("v", lambda: g.vector.tensor_scalar(out, in0, s1, None, op0), rd, wr)
        else:
            do("v", lambda: g.vector.tensor_scalar(out, in0, s1, s2, op0, op1), rd, wr)

    def tt(out, a, b, op, rd, wr):
        do("v", lambda: g.vector.tensor_tensor(out, a, b, op), rd, wr)

    def fill(b, c0, c1, v):
        do("v", lambda: g.vector.memset(T[b][:, c0:c1], v), [], [rg(b, c0, c1)])

    def tr(ob, o0, ib, i0, n):
        do("v", lambda: g.vector.transpose(T[ob][:, o0:o0 + n], T[ib][:, i0:i0 + n]), [rg(ib, i0, i0 + n)], [rg(ob, o0, o0 + n)])

    def pick_codes(ob, o0, ib, n, lb, l0, k):
        c, oc = ib + "c", ob + "c"
        do("v", lambda: g.vector.tensor_copy(T[oc][:, o0:o0 + k].bitcast(dt.uint32), T[c][:, 0:n].bitcast(dt.uint32).indirect(T[lb][:, l0:l0 + k // 16])),
           [rg(c, 0, n), rg(lb, l0, l0 + k // 16)], [rg(oc, o0, o0 + k)])

    def pick_scales(ob, o0, ib, n, lb, l0, k):
        s, os_ = ib + "s", ob + "s"
        do("s", lambda: g.scalar.activation(T[os_][:, o0:o0 + k], T[s][:, 0:n].indirect(T[lb][:, l0:l0 + k // 16]), AF.Copy),
           [rg(s, 0, n), rg(lb, l0, l0 + k // 16)], [rg(os_, o0, o0 + k)])

    def mm(bank, lc, l0, rc, r0, n):
        lh, ls, rh, rs = T[lc + "c"], T[lc + "s"], T[rc + "c"], T[rc + "s"]
        do("t", lambda: g.tensor.matmul_mx(T[bank][:, 0:n], lh[:, l0:l0 + 128], ls[:, l0:l0 + 128], rh[:, r0:r0 + n], rs[:, r0:r0 + n], True, True),
           [rg(lc + "c", l0, l0 + 128), rg(lc + "s", l0, l0 + 128), rg(rc + "c", r0, r0 + n), rg(rc + "s", r0, r0 + n)], [rg(bank, 0, 512)])

    def quantize(ob, o0, n, ib):
        c, s = T[ob + "c"], T[ob + "s"]
        do("v", lambda: g.vector.quantize_mx(c[:, o0:o0 + n], s[:, o0:o0 + n], T[ib][:, 4 * o0:4 * (o0 + n)]),
           [rg(ib, 4 * o0, 4 * (o0 + n))], [rg(ob + "c", o0, o0 + n), rg(ob + "s", o0, o0 + n)])

    def square(ob, o0, bank, i0, n):
        do("s", lambda: g.scalar.activation(T[ob][:, o0:o0 + n], T[bank][:, i0:i0 + n], AF.Square), [rg(bank, 0, 512)], [rg(ob, o0, o0 + n)])

    def lift(c0, c1):
        ts(T.wc[:, c0:c1], T.wr[:, c0:c1], EPS, None, A.max, None, [rg("wr", c0, c1)], [rg("wc", c0, c1)])

    def copy_slots(frm, to, c0, c1):
        for k in ("c", "s"):
            a, b = frm + k, to + k
            i, o = T[a][:, c0:c1], T[b][:, c0:c1]
            if k == "c":
                i, o = i.bitcast(dt.uint8), o.bitcast(dt.uint8)
            dma("y", o, i, [rg(a, c0, c1)], [rg(b, c0, c1)])

    def turn(t):
        tb, sr = ("tsb" if t < 3 else "tsf"), "srow%d" % t
        tr(tb, 0, sr, 16, 128)
        tr(tb, 128, sr, 0, 160)
        return tb

    def in_order(out, wr, src, n, k):
        ts(out, T[src][:, 0:n].indirect(T.co[:, k:k + 1]), 256.0, None, A.add, None, [rg(src, 0, n), rg("co", k, k + 1)], wr)

    def iota(b, c0, c1, pattern, base, cm, p0=0, p1=128):
        do("g", lambda: g.iota(T[b][p0:p1, c0:c1], pattern, base, cm, allow_small_or_imprecise_dtypes=True), [], [rg(b, c0, c1, p0, p1)])

    def g_tables(u):
        iota("cw%d" % u, 0, 272, [[0, 272]], -1000, 0)
        iota("cw%d" % u, 16, 112, [[1, K]], NS[u] - 256, 0)
        iota("win%d" % u, 0, 128, [[0, 128]], 0, 0)

    def g_pads(u):
        for c in (0, 144):
            iota("srow%d" % u, c, c + 16, [[0, 16]], 0, 0)

    for h in range(2):
        dma("y", T.cb[:, 2 * P * h:2 * P * h + 2 * P], T.c[:, 2 * P * h:2 * P * h + 2 * P], [], [rg("cb", 2 * P * h, 2 * P * h + 2 * P)])
    dma("s", T.qb[:, 0:16], T.qt[:, 0:16], [], [rg("qb", 0, 16)])
    dma("y", T.wb[:], T.w[:], [rg("cb", 0, 4 * P)], [rg("wb", 0, 512 * O)])
    fill("cz", 0, 96, 0.0)
    fill("qb", 16, 512, 0.0)
    for t in range(R):
        fill("qoff", 8 * t, 8 * t + 8, t)
    fill("srow0", 0, 16, 0.0)
    fill("srow0", 144, 160, 0.0)
    fill("win0", 0, 128, 0.0)
    fill("cw0", 0, 272, -1000.0)
    for a in range(4):
        iota("s8", 0, 8, [[128 * (1 - 2 * (a // 2)), 2], [64 * (1 - 2 * (a % 2)), 2], [1, 2]], 64 * a, 2, 32 * a, 32 * a + 32)
    iota("iot", 0, P, [[1, P]], -256, 0)
    iota("cz", 0, 16, [[32, 4], [160, 2], [16, 2]], 0, 0)
    iota("cz", 16, 32, [[32, 4], [-128, 2], [16, 2]], 128, 0)
    iota("p2", 0, 1, [[0, 1]], -256, 2)

    quantize("q", 0, 128, "qb")
    for t in range(R):
        pick_scales("qr", 128 * t, "q", 128, "qoff", 8 * t, 128)
    pick_codes("qr", 0, "q", 128, "qoff", 0, 128)
    cp("v", "hl", (0, 8), "s8", (0, 8))
    do("v", lambda: g.vector.tensor_copy(T.srow0[:, 16:144], T.iot[:, 0:P].indirect(T.hl[:, 0:8])), [rg("iot", 0, P), rg("hl", 0, 8)], [rg("srow0", 16, 144)])
    tw = turn(0)
    tr("ctr", 0, "cz", 0, 32)
    cp("v", "co", (0, 1), "ctr", (0, 1))
    in_order(T.fl[:, 0:16], [rg("fl", 0, 16)], tw, 288, 0)
    do("s", lambda: g.scalar.activation(T.pr[:, 0:P], T.iot[:, 0:P].indirect(T.fl[:, 0:16]), AF.Copy), [rg("iot", 0, P), rg("fl", 0, 16)], [rg("pr", 0, P)])
    for h in range(2):
        quantize("w0", 128 * h, 128, "cb")
        mm("ps%d" % h, "qr", 0, "w0", 128 * h, 128)
        square("wr", 128 * h, "ps%d" % h, 0, 128)
    send_codes(0, "h", 0, "w0", P)
    iota("cz", 32, 38, [[1, 3], [4, 2]], 0, 0)
    iota("cz", 48, 54, [[1, 3], [-3, 2]], 3, 0)
    iota("cz", 64, 80, [[160, 2], [32, 4], [16, 2]], 0, 0)
    iota("cz", 80, 96, [[-128, 2], [32, 4], [16, 2]], 128, 0)
    iota("cw0", 16, 112, [[1, K]], NS[0] - 256, 0)
    g_pads(1)
    pick_codes("qr", 128, "q", 128, "qoff", 8, 128)
    ts(T.mm[:, 0:P], T.pr[:, 0:P], T.p2[:, 0:1], 1.0 - 2.0 ** -24, A.is_gt, A.max, [rg("pr", 0, P), rg("p2", 0, 1)], [rg("mm", 0, P)])
    for h in range(2):
        lift(128 * h, 128 * h + 128)

    def y_gather(q, t, o, h):
        n = NS[t + 1]
        b, s, f = "yb%d" % t, "yp%d" % o, "fy%d" % t
        out = T[b][:, P * o + h:P * o + P:2]
        win = T[s][:, 0:n].indirect(T[f][:, 8 * h:8 * h + 8])
        rd, wr = [rg(s, 0, n), rg(f, 8 * h, 8 * h + 8)], [rg(b, P * o, P * o + P, 0, 128, h)]
        if q == "v":
            do("v", lambda: g.vector.tensor_copy(out, win), rd, wr)
        else:
            do("s", lambda: g.scalar.activation(out, win, AF.Copy), rd, wr)

    def y_store(t, o0, o1):
        dma("y", T.y[:, P * (O * t + o0):P * (O * t + o1)], T["yb%d" % t][:, P * o0:P * o1], [rg("yb%d" % t, P * o0, P * o1)], [])

    def new_products(t):
        for o in range(O):
            mm("ps%d" % (2 + o), "wt", 128 * o, "w%d" % (t + 1), NS[t] - 32 if t < 3 else 0, 128)

    def new_copy(t, q, o):
        cp(q, "yp%d" % o, (NS[t], NS[t + 1]), "ps%d" % (2 + o), (32, 128))

    for t in range(R):
        n = NS[t]
        wn, tb, sr, cw, ls = "win%d" % t, ("ttb" if t < 3 else "ttf"), "srow%d" % t, "cw%d" % t, "lst%d" % t
        do("s", lambda: g.scalar.activation(T.u64[:, 0:64], T.wc[:, 0:n].indirect(T.fl[:, 0:4]), AF.Copy), [rg("wc", 0, n), rg("fl", 0, 16)], [rg("u64", 0, 64)])
        if t == 1:
            for o in range(O):
                cp("s", "yp%d" % o, (0, P), "ps%d" % (5 + o), (0, P))
        elif t > 1:
            for o in range(O):
                new_copy(t - 1, "s", o)
        tt(T.rr[:, 0:P], T.wc[:, 0:n].indirect(T.fl[:, 0:16]), T.mm[:, 0:P], A.mult, [rg("wc", 0, n), rg("fl", 0, 16), rg("mm", 0, P)], [rg("rr", 0, P)])
        tr("t4", 0, "u64", 0, 64)
        for e in range(2):
            ts(T["c%d" % e][:, 0:P], T.rr[:, 0:P], T.t4[:, 32 * e:32 * e + 1], None, A.is_lt, None, [rg("rr", 0, P), rg("t4", 32 * e, 32 * e + 1)], [rg("c%d" % e, 0, P)])
        for e in range(2):
            do("v", lambda: g.vector.tensor_tensor_scan(T.kk[:, 128 * e:128 * e + 128], T["c%d" % e][:, 0:128], T["c%d" % e][:, 128:256], float(e - 1), A.add, A.add),
               [rg("c%d" % e, 0, P)], [rg("kk", 128 * e, 128 * e + 128)])
        cnt = (127, 256, 128)
        cp("v", "r8", (2, 4), "kk", cnt, (64, 96), (96, 128))
        cp("s", "r8", (2, 4), "kk", cnt, (0, 32), (32, 64))
        cp("v", "r8", (2, 4), "kk", cnt, (96, 128), (64, 96))
        cp("s", "r8", (2, 4), "kk", cnt, (32, 64), (0, 32))
        cp("v", "r8", (0, 2), "kk", cnt)
        if t == 0:
            tr("ctr", 32, "cz", 32, 64)
        for o0, o1, i0, i1, c in ((0, 64, 64, 128, 4), (64, 128, 0, 64, 4), (0, 128, 0, 128, 0)):
            ts(T.off[o0:o1, c:c + 4], T.r8[i0:i1, 0:4], 16.0, None, A.add, None, [rg("r8", 0, 4, i0, i1)], [rg("off", c, c + 4, o0, o1)])
        if t == 1:
            for o in range(O):
                new_copy(0, "s", o)
        for o, h in (((0, 0),) if t == 1 else ((0, 0), (0, 1), (1, 0)) if t > 1 else ()):
            y_gather("s", t - 1, o, h)
        if t == 0:
            cp("v", "co", (2, 6, 2), "ctr", (32, 96, 32))
        do("v", lambda: g.vector.tensor_copy(T[wn][:, 0:272].indirect(T.off[:, 0:8]), T[sr][:, 16:144]), [rg(sr, 16, 144), rg("off", 0, 8)], [rg(wn, 0, 272)])
        tr(tb, 0, wn, 16, 96)
        tr(tb, 96, wn, 0, 128)
        tt(T.a7[:, 0:7], T[tb][:, 0:224:32], T[tb][:, 16:224:32], A.add, [rg(tb, 0, 224)], [rg("a7", 0, 7)])
        in_order(T[ls][:, 0:16], [rg(ls, 0, 16)], "a7", 7, 2)
        nx = "w%d" % (t + 1)
        if t == 0:
            send(0, T.alst[:, 0:6], T.lst0[:, 0:6], [rg("lst0", 0, 6)], [rg("alst", 0, 6)], "al", "ll")
        else:
            pick_codes("out%d" % t, 0, "w%d" % t, n, ls, 0, K)
            pick_scales("out%d" % t, 0, "w%d" % t, n, ls, 0, K)
            send_codes(t, nx, n if t < 3 else 32, "out%d" % t, K)

        if t == 1:
            pick_codes("qr", 256, "q", 128, "qoff", 16, 128)
        if t < 3:
            mm("ps0", "qr", 128 * (t + 1), "w%d" % t, 0, n)
            square("sq", 0, "ps0", 0, n)
        if t == 0:
            mm("ps1", "qr", 128, "h", 0, P)
            square("hq", 0, "ps1", 0, P)
        if t < 3:
            g_tables(t + 1)
            g_pads(t + 2)
        sn = "srow%d" % (t + 1)
        tt(T[sn][:, 16:144], T[cw][:, 0:272].indirect(T.off[:, 0:8]), T[sr][:, 16:144], A.max, [rg(cw, 0, 272), rg("off", 0, 8), rg(sr, 16, 144)], [rg(sn, 16, 144)])
        tw = turn(t + 1)
        if t < 3:
            in_order(T.fl[:, 0:16], [rg("fl", 0, 16)], tw, 288, 0)
        fy = "fy%d" % t
        in_order(T[fy][:, 0:16], [rg(fy, 0, 16)], tw, 288, 4)
        if t < 3:
            for a in range(1, 4):
                dma("y", T[fy][32 * a:32 * a + 32, 0:16], T[fy][0:32, 0:16], [rg(fy, 0, 16, 0, 32)], [rg(fy, 0, 16, 32 * a, 32 * a + 32)])
            tt(T.wr[:, 0:n], T.wr[:, 0:n], T.sq[:, 0:n], A.add, [rg("wr", 0, n), rg("sq", 0, n)], [rg("wr", 0, n)])
            lift(0, n)
        else:
            for a in range(1, 4):
                cp("v", fy, (0, 16), fy, (0, 16), (32 * a, 32 * a + 32), (0, 32))
        if t == 0:
            for o in range(O):
                quantize("wt", 128 * o, 128, "wb")
                mm("ps%d" % (5 + o), "wt", 128 * o, "w0", 0, P)
            copy_slots("w0", "w1", 0, P)
            copy_slots("w0", "w4", 0, 32)
        elif t == 1:
            pick_codes("qr", 384, "q", 128, "qoff", 24, 128)
            for o, h in ((0, 1), (1, 0), (1, 1), (2, 0), (2, 1)):
                y_gather("s", 0, o, h)
        else:
            if t == 3:
                y_store(2, 0, 1)
            for o, h in ((1, 1), (2, 0), (2, 1)):
                y_gather("s", t - 1, o, h)
            if t == 3:
                y_store(2, 1, 3)
        if t < 3:
            if t == 0:
                do("s", lambda: g.scalar.activation(T.wr[:, n:n + K], T.hq[:, 0:P].indirect(T.alst[:, 0:6]), AF.Copy), [rg("hq", 0, P), rg("alst", 0, 6)], [rg("wr", n, n + K)])
                pick_codes("w1", n, "h", P, "alst", 0, K)
                pick_scales("w1", n, "h", P, "alst", 0, K)
            else:
                mm("ps1", "qr", 128 * (t + 1), nx, n - 32, 128)
                square("wr", n, "ps1", 32, K)
            lift(n, n + K)
            if t == 0:
                for u in range(2, R):
                    copy_slots("w0", "w%d" % u, 0, P)
            for u in range(t + 2, R):
                copy_slots(nx, "w%d" % u, n, n + K)
            if t > 0:
                y_store(t - 1, 0, O)
        new_products(t)
    new_copy(3, "s", 0)
    y_gather("s", 3, 0, 0)
    y_gather("v", 3, 0, 1)
    new_copy(3, "v", 1)
    new_copy(3, "s", 2)
    y_gather("v", 3, 1, 0)
    y_gather("s", 3, 1, 1)
    y_gather("v", 3, 2, 0)
    y_gather("s", 3, 2, 1)
    for o in range(O):
        y_store(3, o, o + 1)

    for sem in count:
        if waited["g"].get(sem, 0) < count[sem]:
            g.wait_ge(T.sem[sem], count[sem])
